import numpy as np
import ml_dtypes


def mxq(x, axis, fmt="e4m3"):
    dtype, down = {"e4m3": (ml_dtypes.float8_e4m3fn, 7), "e5m2": (ml_dtypes.float8_e5m2, 14)}[fmt]
    v = np.moveaxis(np.asarray(x, np.float32).astype(ml_dtypes.bfloat16).astype(np.float64), axis, -1)
    blocks = v.reshape(v.shape[:-1] + (-1, 32))
    amax = np.abs(blocks).max(-1, keepdims=True)
    byte = np.maximum(np.where(amax > 0, np.frexp(amax)[1] - 1 + 127, 0) - down, 1)
    scale = np.exp2(byte - 127.0)
    codes = (blocks / scale).astype(np.float32).astype(dtype).astype(np.float64)
    return np.moveaxis((codes * scale).reshape(v.shape), -1, axis)


WIDE = False


def mx_kscale(k):
    if not WIDE:
        return np.ones(k)
    levels = np.array([10, -10, 5, -5, 0])
    if k % 512:
        return np.exp2(np.random.permutation(np.resize(levels, k // 32))).repeat(32)
    a = np.empty((k // 512, 16))
    for p in range(k // 512):
        a[p, :8] = np.random.permutation(np.resize(levels, 8))
        for g in range(8):
            far = levels[np.abs(levels - a[p, g]) >= 10]
            a[p, g + 8] = far[np.random.randint(len(far))]
    return np.exp2(a.ravel()).repeat(32)


def f64(x):
    return np.asarray(x).astype(np.float64)


def striped(idx):
    return np.tile(idx.reshape(-1, 16).T, (8, 1)).astype(np.uint16)


def unstriped(offs):
    return offs[:16].T.reshape(-1).astype(np.int64)


E2M1 = np.array([0.0, 0.5, 1.0, 1.5, 2.0, 3.0, 4.0, 6.0, -0.0, -0.5, -1.0, -1.5, -2.0, -3.0, -4.0, -6.0])


def pack_weight(w, fmt):
    k, n = w.shape
    w = f64(np.asarray(w, np.float32).astype(ml_dtypes.bfloat16)).reshape(k // 32, 32, n)
    amax = np.abs(w).max(1)
    if fmt == "e4m3":
        byte = np.frexp(amax)[1] - 1 + 127 - 7
    else:
        mant, ex = np.frexp(amax / 6.0)
        byte = np.where(mant > 0.5, ex, ex - 1) + 127
    byte = np.clip(np.where(amax > 0, byte, 1), 1, 254)
    scaled = (w * np.exp2(127.0 - byte)[:, None, :]).reshape(k, n).astype(np.float32)
    by_word = np.ascontiguousarray(scaled.reshape(k // 512, 128, 4, n).transpose(0, 1, 3, 2))
    if fmt == "e4m3":
        words = by_word.astype(ml_dtypes.float8_e4m3fn).view(np.uint8)
    else:
        c = by_word.astype(ml_dtypes.float4_e2m1fn).view(np.uint8) & 0xF
        words = (c[..., 0::2] | (c[..., 1::2] << 4)).reshape(k // 512, 128, 2 * n)
    return np.ascontiguousarray(words), np.ascontiguousarray(byte.astype(np.uint8).reshape(k // 512, 16, n))


def unpack_weight(words, scales, fmt):
    g, _, n = scales.shape
    words = np.ascontiguousarray(words).reshape(g, 128, n, -1)
    if fmt == "e4m3":
        vals = words.view(ml_dtypes.float8_e4m3fn).astype(np.float64)
    else:
        nib = np.empty((g, 128, n, 4), np.uint8)
        nib[..., 0::2] = words & 0xF
        nib[..., 1::2] = words >> 4
        vals = E2M1[nib]
    vals = vals * np.repeat(np.exp2(scales.astype(np.float64) - 127.0), 8, axis=1)[..., None]
    return vals.transpose(0, 1, 3, 2).reshape(g * 512, n)


def gelu(v):
    return 0.5 * v * (1.0 + np.tanh(np.sqrt(2.0 / np.pi) * (v + 0.044715 * v**3)))


K, H, N, T, S = 512, 1024, 768, 2048, 1024


def setup_inputs():
    n = np.random.standard_normal
    s = mx_kscale(K)[:, None]
    u = mx_kscale(H)[:, None]
    tab_words, tab_scales = pack_weight(n((K, T)) * s, "e4m3")
    w1 = n((K, H)) / np.sqrt(K) / s * u.T
    w4_words, w4_scales = pack_weight(n((H, N)) / np.sqrt(H) / u, "e2m1")
    gT = np.exp(0.5 * n((1, T)) + 0.3 * n((N, T)))
    return {
        "tab_words": tab_words, "tab_scales": tab_scales,
        "offs": striped(np.random.permutation(T)[:S]),
        "w1": w1.astype(np.float32),
        "w4_words": w4_words, "w4_scales": w4_scales,
        "gT": gT.astype(np.float32),
    }


def reference(tab_words, tab_scales, offs, w1, w4_words, w4_scales, gT):
    v = unpack_weight(tab_words, tab_scales, "e4m3")[:, unstriped(offs)]
    g = f64(gT)[:, unstriped(offs)]
    w1q = mxq(f64(w1), 0, "e4m3")
    w4 = unpack_weight(w4_words, w4_scales, "e2m1")
    h = np.maximum(w1q.T @ v, 0.0)
    hq = mxq(h, 0, "e4m3")
    y = w4.T @ hq
    mu = g * np.exp(y)
    return np.log(1.0 + mu)

@@ -1,0 +1,223 @@
+from contextlib import ExitStack
+
+import concourse.mybir as mybir
+
+K, H, N, T, S = 512, 1024, 768, 2048, 1024
+FLOPS = 2 * K * H * S + 2 * H * N * S
+
+F32 = mybir.dt.float32
+BF16 = mybir.dt.bfloat16
+I32 = mybir.dt.int32
+U32 = mybir.dt.uint32
+U16 = mybir.dt.uint16
+U8 = mybir.dt.uint8
+FP8X4 = mybir.dt.float8_e4m3fn_x4
+FP4X4 = mybir.dt.float4_e2m1fn_x4
+ACT = mybir.ActivationFunctionType
+ALU = mybir.AluOpType
+
+P = 128
+PACK = 4
+K_PASS = P * PACK
+PASSES = H // K_PASS
+GENE_TILES = N // P
+HALF = 512
+QUAD = 128
+
+
+def tile_list_barcode_log_expression_kernel(tc, tab_words, tab_scales, offs, w1, w4_words, w4_scales, gT, out):
+    nc = tc.nc
+    with ExitStack() as ctx:
+        keep = ctx.enter_context(tc.tile_pool(name="keep", bufs=1))
+        psum_h = ctx.enter_context(tc.psum_pool(name="psum_h", bufs=4))
+        psum_y = ctx.enter_context(tc.psum_pool(name="psum_y", bufs=4))
+
+        offsets = keep.tile([P, S // 16], U16, name="offsets")
+        table = keep.tile([P, T], U32, name="table", align_bytes=64)
+        table_sc = keep.tile([P, T], U8, name="table_sc", align_bytes=64)
+        w1_raw = [keep.tile([P, PACK, K_PASS], F32, name="w1_raw%d" % b, align_bytes=64) for b in range(PASSES)]
+        w1_bf = [keep.tile([P, PACK * K_PASS], BF16, name="w1_bf%d" % b, align_bytes=64) for b in range(PASSES)]
+        w1_q = [keep.tile([P, K_PASS], U32, name="w1_q%d" % b, align_bytes=64) for b in range(PASSES)]
+        w1_sc = [keep.tile([P, K_PASS], U8, name="w1_sc%d" % b, align_bytes=64) for b in range(PASSES)]
+        w4 = keep.tile([P, PASSES, 2 * N], U8, name="w4", align_bytes=64)
+        w4_sc = keep.tile([P, PASSES, N], U8, name="w4_sc", align_bytes=64)
+        g = [keep.tile([P, T], F32, name="g%d" % n, align_bytes=64) for n in range(GENE_TILES)]
+        v_q = keep.tile([P, S], U32, name="v_q", align_bytes=64)
+        v_sc = keep.tile([P, S], U8, name="v_sc", align_bytes=64)
+        h_bf = keep.tile([P, PASSES, S * PACK], BF16, name="h_bf", align_bytes=64)
+        h_q = keep.tile([P, PASSES, S], U32, name="h_q", align_bytes=64)
+        h_sc = keep.tile([P, PASSES, S], U8, name="h_sc", align_bytes=64)
+        rate = keep.tile([P, GENE_TILES, S], F32, name="rate", align_bytes=64)
+        count = keep.tile([P, GENE_TILES, S], F32, name="count", align_bytes=64)
+        res = keep.tile([P, GENE_TILES, S], F32, name="res", align_bytes=64)
+        zero = keep.tile([P, 1], F32, name="zero")
+        one_early = keep.tile([P, 1], F32, name="one_early")
+        one_late = keep.tile([P, GENE_TILES * 2], F32, name="one_late")
+
+        def cells(c0, n):
+            return slice(c0, c0 + n)
+
+        def listed(c0, n):
+            return offsets[:, c0 // 16 : (c0 + n) // 16]
+
+        def load_w1(b):
+            nc.sync.dma_start(w1_raw[b][:], w1.rearrange("(p j) c -> p j c", j=PACK)[:, :, b * K_PASS : (b + 1) * K_PASS])
+
+        def load_w1_part(b, j0, nj, c0, ncol):
+            src = w1.rearrange("(p j) c -> p j c", j=PACK)
+            nc.sync.dma_start(w1_raw[b][:, j0 : j0 + nj, c0 : c0 + ncol],
+                              src[:, j0 : j0 + nj, b * K_PASS + c0 : b * K_PASS + c0 + ncol])
+
+        def cast_w1_part(b, m0, nm, eng):
+            dst = w1_bf[b][:].rearrange("p (t m j) -> p m j t", t=PACK, j=PACK)[:, m0 : m0 + nm]
+            src = w1_raw[b][:].rearrange("p j (m t) -> p m j t", t=PACK)[:, m0 : m0 + nm]
+            if eng == "S":
+                nc.scalar.copy(dst, src)
+            elif eng == "V":
+                nc.vector.tensor_copy(dst, src)
+            else:
+                nc.gpsimd.tensor_scalar(dst, src, 1.0, 0.0, ALU.mult, ALU.add)
+
+        def load_table():
+            nc.sync.dma_start(table[:].bitcast(I32), tab_words[0].rearrange("p t i -> p (t i)").bitcast(I32))
+
+        def load_table_sc(eng):
+            rows = tab_scales[0].rearrange("(q r) t -> r q t", r=4)
+            for r in range(4):
+                eng.dma_start(table_sc[:].bitcast(I32)[r:P:32, :], rows[r].bitcast(I32))
+
+        def load_w4():
+            rows = w4_scales.rearrange("a (q r) c -> r q a c", r=4)
+            for r in range(4):
+                nc.sync.dma_start(w4_sc[:].bitcast(I32)[r:P:32, :, :], rows[r].bitcast(I32))
+            nc.sync.dma_start(w4[:].bitcast(I32), w4_words.rearrange("a p c -> p a c").bitcast(I32))
+
+        def cast_w1(b, eng):
+            dst = w1_bf[b][:].rearrange("p (t m j) -> p m j t", t=PACK, j=PACK)
+            src = w1_raw[b][:].rearrange("p j (m t) -> p m j t", t=PACK)
+            if eng == "S":
+                nc.scalar.copy(dst, src)
+            elif eng == "V":
+                nc.vector.tensor_copy(dst, src)
+            else:
+                nc.gpsimd.tensor_scalar(dst, src, 1.0, 0.0, ALU.mult, ALU.add)
+
+        def quant_w1(b):
+            nc.vector.quantize_mx(w1_q[b][:].bitcast(FP8X4), w1_sc[b][:], w1_bf[b][:])
+
+        def gather_words(c0, n):
+            nc.vector.tensor_copy(v_q[:, cells(c0, n)], table[:].indirect(listed(c0, n)))
+
+        def gather_scales(c0, n):
+            nc.vector.tensor_copy(v_sc[:, cells(c0, n)], table_sc[:].indirect(listed(c0, n)))
+
+        def hidden(b, q, eng):
+            acc = psum_h.tile([P, PACK, QUAD], F32, name="acc_h")
+            cs = cells(q * QUAD, QUAD)
+            for t in range(PACK):
+                ms = cells(t * P, P)
+                nc.tensor.matmul_mx(acc[:, t, :], lhsT=w1_q[b][:, ms].bitcast(FP8X4), lhsT_scale=w1_sc[b][:, ms],
+                                    rhs=v_q[:, cs].bitcast(FP8X4), rhs_scale=v_sc[:, cs], start=True, stop=True)
+            dst = h_bf[:, b, cells(q * QUAD * PACK, QUAD * PACK)].rearrange("p (c t) -> p c t", t=PACK)
+            src = acc[:].rearrange("p t c -> p c t")
+            if eng == "S":
+                nc.scalar.activation(dst, src, ACT.Relu)
+            else:
+                nc.vector.tensor_scalar_max(dst, src, 0.0)
+
+        def quant_h(b, c0, n):
+            nc.vector.quantize_mx(h_q[:, b, cells(c0, n)].bitcast(FP8X4), h_sc[:, b, cells(c0, n)],
+                                  h_bf[:, b, cells(c0 * PACK, n * PACK)])
+
+        def rates(n, c):
+            acc = psum_y.tile([P, HALF], F32, name="acc_y")
+            cs = cells(c * HALF, HALF)
+            for b in range(PASSES):
+                nc.tensor.matmul_mx(acc[:], lhsT=w4[:, b, cells(n * 2 * P, 2 * P)].bitcast(FP4X4),
+                                    lhsT_scale=w4_sc[:, b, cells(n * P, P)],
+                                    rhs=h_q[:, b, cs].bitcast(FP8X4), rhs_scale=h_sc[:, b, cs],
+                                    start=(b == 0), stop=(b == PASSES - 1))
+            nc.scalar.activation(rate[:, n, cs], acc[:], ACT.Exp)
+
+        def counts(n, c0, w):
+            nc.vector.tensor_tensor(count[:, n, cells(c0, w)], g[n][:].indirect(listed(c0, w)), rate[:, n, cells(c0, w)], ALU.mult)
+
+        def finish(n, c0, w):
+            cs = cells(c0, w)
+            nc.scalar.activation(res[:, n, cs], count[:, n, cs], ACT.Ln, bias=one_late[:, 0:1])
+            nc.sync.dma_start(out[n * P : (n + 1) * P, cs], res[:, n, cs])
+
+        def gate_ln():
+            nc.scalar.activation(one_late[:].rearrange("p (n c) -> p n c", c=2), rate[:, :, HALF - 1 : S : HALF], ACT.Sign, bias=one_early[:])
+
+        nc.vector.memset(table_sc[:].bitcast(I32), 0)
+        nc.vector.memset(zero[:], 0.0)
+        nc.vector.memset(w4_sc[:].bitcast(I32), 0)
+        nc.scalar.activation(one_early[:], zero[:], ACT.Exp)
+
+        nc.sync.dma_start(offsets[:], offs)
+        load_w1_part(0, 0, 2, 0, 256)
+        load_w1_part(0, 2, 2, 0, 256)
+        load_table_sc(nc.sync)
+        load_w1_part(0, 0, 4, 256, 256)
+        load_table()
+        load_w1(1)
+        load_w4()
+        for n in range(GENE_TILES):
+            nc.sync.dma_start(g[n][:], gT[n * P : (n + 1) * P, :])
+
+        cast_w1_part(0, 0, 64, "S")
+        cast_w1_part(0, 64, 64, "S")
+        gather_scales(0, 512)
+        gather_scales(512, 512)
+        quant_w1(0)
+        gather_words(0, 256)
+        gather_words(256, 256)
+        gather_words(512, 512)
+        for q in range(4):
+            hidden(0, q, "S")
+        cast_w1(1, "V")
+        quant_w1(1)
+        quant_h(0, 0, 512)
+        hidden(0, 4, "S")
+        hidden(0, 5, "S")
+        hidden(0, 6, "S")
+        hidden(1, 0, "S")
+        hidden(1, 1, "V")
+        hidden(1, 2, "S")
+        hidden(1, 3, "V")
+        quant_h(1, 0, 512)
+        hidden(0, 7, "S")
+        hidden(1, 4, "S")
+        hidden(1, 5, "S")
+        quant_h(0, 512, 512)
+        hidden(1, 6, "V")
+        rates(0, 0)
+        hidden(1, 7, "S")
+        counts(0, 0, 512)
+        quant_h(1, 512, 512)
+        rates(1, 0)
+        rates(2, 0)
+        counts(1, 0, 512)
+        rates(3, 0)
+        counts(2, 0, 512)
+        rates(4, 0)
+        rates(5, 0)
+        for n in range(GENE_TILES):
+            rates(n, 1)
+        gate_ln()
+        counts(0, 512, 512)
+        counts(3, 0, 512)
+        counts(1, 512, 512)
+        counts(2, 512, 512)
+        counts(3, 512, 512)
+        counts(4, 0, 512)
+        counts(4, 512, 512)
+        counts(5, 0, 512)
+        counts(5, 512, 256)
+        counts(5, 768, 256)
+        for n in range(GENE_TILES - 1):
+            finish(n, 0, 1024)
+        finish(5, 0, 512)
+        finish(5, 512, 256)
+        finish(5, 768, 256)

@@ -29,8 +29,7 @@ def tile_list_barcode_log_expression_kernel(tc, tab_words, tab_scales, offs, w1,
     nc = tc.nc
     with ExitStack() as ctx:
         keep = ctx.enter_context(tc.tile_pool(name="keep", bufs=1))
-        psum_h = ctx.enter_context(tc.psum_pool(name="psum_h", bufs=4))
-        psum_y = ctx.enter_context(tc.psum_pool(name="psum_y", bufs=4))
+        psum = ctx.enter_context(tc.psum_pool(name="psum", bufs=8))
 
         offsets = keep.tile([P, S // 16], U16, name="offsets")
         table = keep.tile([P, T], U32, name="table", align_bytes=64)
@@ -52,7 +51,7 @@ def tile_list_barcode_log_expression_kernel(tc, tab_words, tab_scales, offs, w1,
         res = keep.tile([P, GENE_TILES, S], F32, name="res", align_bytes=64)
         zero = keep.tile([P, 1], F32, name="zero")
         one_early = keep.tile([P, 1], F32, name="one_early")
-        one_late = keep.tile([P, GENE_TILES * 2], F32, name="one_late")
+        one_late = keep.tile([P, GENE_TILES * 2 - 1], F32, name="one_late")
 
         def cells(c0, n):
             return slice(c0, c0 + n)
@@ -112,7 +111,7 @@ def tile_list_barcode_log_expression_kernel(tc, tab_words, tab_scales, offs, w1,
             nc.vector.tensor_copy(v_sc[:, cells(c0, n)], table_sc[:].indirect(listed(c0, n)))
 
         def hidden(b, q, eng):
-            acc = psum_h.tile([P, PACK, QUAD], F32, name="acc_h")
+            acc = psum.tile([P, PACK, QUAD], F32, name="acc_h", tag="bank")
             cs = cells(q * QUAD, QUAD)
             for t in range(PACK):
                 ms = cells(t * P, P)
@@ -130,7 +129,7 @@ def tile_list_barcode_log_expression_kernel(tc, tab_words, tab_scales, offs, w1,
                                   h_bf[:, b, cells(c0 * PACK, n * PACK)])
 
         def rates(n, c):
-            acc = psum_y.tile([P, HALF], F32, name="acc_y")
+            acc = psum.tile([P, HALF], F32, name="acc_y", tag="bank")
             cs = cells(c * HALF, HALF)
             for b in range(PASSES):
                 nc.tensor.matmul_mx(acc[:], lhsT=w4[:, b, cells(n * 2 * P, 2 * P)].bitcast(FP4X4),
@@ -148,7 +147,8 @@ def tile_list_barcode_log_expression_kernel(tc, tab_words, tab_scales, offs, w1,
             nc.sync.dma_start(out[n * P : (n + 1) * P, cs], res[:, n, cs])
 
         def gate_ln():
-            nc.scalar.activation(one_late[:].rearrange("p (n c) -> p n c", c=2), rate[:, :, HALF - 1 : S : HALF], ACT.Sign, bias=one_early[:])
+            ends = rate[:].rearrange("p n c -> p (n c)")[:, HALF - 1 : GENE_TILES * S - HALF : HALF]
+            nc.scalar.activation(one_late[:], ends, ACT.Sign, bias=one_early[:])
 
         nc.vector.memset(table_sc[:].bitcast(I32), 0)
         nc.vector.memset(zero[:], 0.0)
@@ -156,63 +156,64 @@ def tile_list_barcode_log_expression_kernel(tc, tab_words, tab_scales, offs, w1,
         nc.scalar.activation(one_early[:], zero[:], ACT.Exp)
 
         nc.sync.dma_start(offsets[:], offs)
-        load_w1_part(0, 0, 2, 0, 256)
-        load_w1_part(0, 2, 2, 0, 256)
+        load_w1_part(0, 0, 4, 0, 256)
         load_table_sc(nc.sync)
         load_w1_part(0, 0, 4, 256, 256)
         load_table()
-        load_w1(1)
+        load_w1_part(1, 0, 4, 0, 256)
+        load_w1_part(1, 0, 4, 256, 256)
         load_w4()
         for n in range(GENE_TILES):
             nc.sync.dma_start(g[n][:], gT[n * P : (n + 1) * P, :])
-
         cast_w1_part(0, 0, 64, "S")
         cast_w1_part(0, 64, 64, "S")
-        gather_scales(0, 512)
-        gather_scales(512, 512)
+        gather_scales(0, 1024)
         quant_w1(0)
         gather_words(0, 256)
         gather_words(256, 256)
         gather_words(512, 512)
-        for q in range(4):
-            hidden(0, q, "S")
-        cast_w1(1, "V")
+        cast_w1_part(1, 0, 64, "S")
+        cast_w1_part(1, 64, 64, "V")
         quant_w1(1)
+        hidden(0, 0, "S")
+        hidden(0, 1, "S")
+        hidden(0, 2, "S")
+        hidden(0, 3, "S")
         quant_h(0, 0, 512)
         hidden(0, 4, "S")
         hidden(0, 5, "S")
         hidden(0, 6, "S")
-        hidden(1, 0, "S")
-        hidden(1, 1, "V")
-        hidden(1, 2, "S")
-        hidden(1, 3, "V")
-        quant_h(1, 0, 512)
         hidden(0, 7, "S")
+        hidden(1, 0, "V")
+        hidden(1, 1, "V")
+        hidden(1, 2, "V")
+        hidden(1, 3, "S")
+        quant_h(1, 0, 512)
+        quant_h(0, 512, 512)
         hidden(1, 4, "S")
         hidden(1, 5, "S")
-        quant_h(0, 512, 512)
-        hidden(1, 6, "V")
-        rates(0, 0)
-        hidden(1, 7, "S")
-        counts(0, 0, 512)
+        hidden(1, 6, "S")
+        hidden(1, 7, "V")
         quant_h(1, 512, 512)
+        rates(0, 0)
         rates(1, 0)
         rates(2, 0)
-        counts(1, 0, 512)
         rates(3, 0)
-        counts(2, 0, 512)
+        rates(0, 1)
+        rates(1, 1)
+        rates(2, 1)
+        rates(3, 1)
         rates(4, 0)
+        rates(4, 1)
         rates(5, 0)
-        for n in range(GENE_TILES):
-            rates(n, 1)
+        rates(5, 1)
         gate_ln()
+        counts(0, 0, 512)
         counts(0, 512, 512)
-        counts(3, 0, 512)
-        counts(1, 512, 512)
-        counts(2, 512, 512)
-        counts(3, 512, 512)
-        counts(4, 0, 512)
-        counts(4, 512, 512)
+        counts(1, 0, 1024)
+        counts(2, 0, 1024)
+        counts(3, 0, 1024)
+        counts(4, 0, 1024)
         counts(5, 0, 512)
         counts(5, 512, 256)
         counts(5, 768, 256)

@@ -29,7 +29,7 @@ def tile_list_barcode_log_expression_kernel(tc, tab_words, tab_scales, offs, w1,
     nc = tc.nc
     with ExitStack() as ctx:
         keep = ctx.enter_context(tc.tile_pool(name="keep", bufs=1))
-        psum = ctx.enter_context(tc.psum_pool(name="psum", bufs=8))
+        psum = ctx.enter_context(tc.psum_pool(name="psum", bufs=1))
 
         offsets = keep.tile([P, S // 16], U16, name="offsets")
         table = keep.tile([P, T], U32, name="table", align_bytes=64)
@@ -75,7 +75,7 @@ def tile_list_barcode_log_expression_kernel(tc, tab_words, tab_scales, offs, w1,
             elif eng == "V":
                 nc.vector.tensor_copy(dst, src)
             else:
-                nc.gpsimd.tensor_scalar(dst, src, 1.0, 0.0, ALU.mult, ALU.add)
+                nc.gpsimd.tensor_scalar(dst.rearrange("p m j t -> p t m j"), src.rearrange("p m j t -> p t m j"), 1.0, 0.0, ALU.mult, ALU.add)
 
         def load_table():
             nc.sync.dma_start(table[:].bitcast(I32), tab_words[0].rearrange("p t i -> p (t i)").bitcast(I32))
@@ -110,8 +110,8 @@ def tile_list_barcode_log_expression_kernel(tc, tab_words, tab_scales, offs, w1,
         def gather_scales(c0, n):
             nc.vector.tensor_copy(v_sc[:, cells(c0, n)], table_sc[:].indirect(listed(c0, n)))
 
-        def hidden(b, q, eng):
-            acc = psum.tile([P, PACK, QUAD], F32, name="acc_h", tag="bank")
+        def hidden(b, q, eng, bank):
+            acc = psum.tile([P, PACK, QUAD], F32, name="acc_h", tag="bank%d" % bank)
             cs = cells(q * QUAD, QUAD)
             for t in range(PACK):
                 ms = cells(t * P, P)
@@ -128,8 +128,8 @@ def tile_list_barcode_log_expression_kernel(tc, tab_words, tab_scales, offs, w1,
             nc.vector.quantize_mx(h_q[:, b, cells(c0, n)].bitcast(FP8X4), h_sc[:, b, cells(c0, n)],
                                   h_bf[:, b, cells(c0 * PACK, n * PACK)])
 
-        def rates(n, c):
-            acc = psum.tile([P, HALF], F32, name="acc_y", tag="bank")
+        def rates(n, c, bank):
+            acc = psum.tile([P, HALF], F32, name="acc_y", tag="bank%d" % bank)
             cs = cells(c * HALF, HALF)
             for b in range(PASSES):
                 nc.tensor.matmul_mx(acc[:], lhsT=w4[:, b, cells(n * 2 * P, 2 * P)].bitcast(FP4X4),
@@ -172,41 +172,42 @@ def tile_list_barcode_log_expression_kernel(tc, tab_words, tab_scales, offs, w1,
         gather_words(0, 256)
         gather_words(256, 256)
         gather_words(512, 512)
-        cast_w1_part(1, 0, 64, "S")
+        cast_w1_part(1, 0, 32, "S")
+        cast_w1_part(1, 32, 32, "G")
         cast_w1_part(1, 64, 64, "V")
         quant_w1(1)
-        hidden(0, 0, "S")
-        hidden(0, 1, "S")
-        hidden(0, 2, "S")
-        hidden(0, 3, "S")
+        hidden(0, 0, "S", 0)
+        hidden(0, 1, "S", 1)
+        hidden(0, 2, "S", 2)
+        hidden(0, 3, "S", 3)
         quant_h(0, 0, 512)
-        hidden(0, 4, "S")
-        hidden(0, 5, "S")
-        hidden(0, 6, "S")
-        hidden(0, 7, "S")
-        hidden(1, 0, "V")
-        hidden(1, 1, "V")
-        hidden(1, 2, "V")
-        hidden(1, 3, "S")
+        hidden(0, 4, "S", 4)
+        hidden(0, 5, "S", 5)
+        hidden(0, 6, "S", 6)
+        hidden(1, 0, "V", 7)
+        hidden(1, 1, "S", 0)
+        hidden(1, 2, "V", 1)
+        hidden(1, 3, "V", 2)
         quant_h(1, 0, 512)
+        hidden(1, 4, "S", 3)
+        hidden(1, 5, "S", 4)
+        hidden(0, 7, "S", 1)
+        hidden(1, 6, "S", 5)
+        hidden(1, 7, "V", 2)
         quant_h(0, 512, 512)
-        hidden(1, 4, "S")
-        hidden(1, 5, "S")
-        hidden(1, 6, "S")
-        hidden(1, 7, "V")
         quant_h(1, 512, 512)
-        rates(0, 0)
-        rates(1, 0)
-        rates(2, 0)
-        rates(3, 0)
-        rates(0, 1)
-        rates(1, 1)
-        rates(2, 1)
-        rates(3, 1)
-        rates(4, 0)
-        rates(4, 1)
-        rates(5, 0)
-        rates(5, 1)
+        rates(0, 0, 6)
+        rates(1, 0, 7)
+        rates(2, 0, 0)
+        rates(3, 0, 3)
+        rates(0, 1, 4)
+        rates(1, 1, 5)
+        rates(2, 1, 1)
+        rates(3, 1, 2)
+        rates(4, 0, 6)
+        rates(4, 1, 7)
+        rates(5, 0, 0)
+        rates(5, 1, 3)
         gate_ln()
         counts(0, 0, 512)
         counts(0, 512, 512)
@@ -216,9 +217,11 @@ def tile_list_barcode_log_expression_kernel(tc, tab_words, tab_scales, offs, w1,
         counts(4, 0, 1024)
         counts(5, 0, 512)
         counts(5, 512, 256)
-        counts(5, 768, 256)
+        counts(5, 768, 128)
+        counts(5, 896, 128)
         for n in range(GENE_TILES - 1):
             finish(n, 0, 1024)
         finish(5, 0, 512)
         finish(5, 512, 256)
-        finish(5, 768, 256)
+        finish(5, 768, 128)
+        finish(5, 896, 128)

@@ -51,7 +51,7 @@ def tile_list_barcode_log_expression_kernel(tc, tab_words, tab_scales, offs, w1,
         res = keep.tile([P, GENE_TILES, S], F32, name="res", align_bytes=64)
         zero = keep.tile([P, 1], F32, name="zero")
         one_early = keep.tile([P, 1], F32, name="one_early")
-        one_late = keep.tile([P, GENE_TILES * 2 - 1], F32, name="one_late")
+        one_late = keep.tile([P, 7], F32, name="one_late")
 
         def cells(c0, n):
             return slice(c0, c0 + n)
@@ -128,6 +128,11 @@ def tile_list_barcode_log_expression_kernel(tc, tab_words, tab_scales, offs, w1,
             nc.vector.quantize_mx(h_q[:, b, cells(c0, n)].bitcast(FP8X4), h_sc[:, b, cells(c0, n)],
                                   h_bf[:, b, cells(c0 * PACK, n * PACK)])
 
+        def rate_of(n, c0, w):
+            if (n, c0) == (1, 0):
+                return count[:, 0, cells(HALF, HALF)]
+            return rate[:, n, cells(c0, w)]
+
         def rates(n, c, bank):
             acc = psum.tile([P, HALF], F32, name="acc_y", tag="bank%d" % bank)
             cs = cells(c * HALF, HALF)
@@ -136,10 +141,10 @@ def tile_list_barcode_log_expression_kernel(tc, tab_words, tab_scales, offs, w1,
                                     lhsT_scale=w4_sc[:, b, cells(n * P, P)],
                                     rhs=h_q[:, b, cs].bitcast(FP8X4), rhs_scale=h_sc[:, b, cs],
                                     start=(b == 0), stop=(b == PASSES - 1))
-            nc.scalar.activation(rate[:, n, cs], acc[:], ACT.Exp)
+            nc.scalar.activation(rate_of(n, c * HALF, HALF), acc[:], ACT.Exp)
 
         def counts(n, c0, w):
-            nc.vector.tensor_tensor(count[:, n, cells(c0, w)], g[n][:].indirect(listed(c0, w)), rate[:, n, cells(c0, w)], ALU.mult)
+            nc.vector.tensor_tensor(count[:, n, cells(c0, w)], g[n][:].indirect(listed(c0, w)), rate_of(n, c0, w), ALU.mult)
 
         def finish(n, c0, w):
             cs = cells(c0, w)
@@ -147,7 +152,7 @@ def tile_list_barcode_log_expression_kernel(tc, tab_words, tab_scales, offs, w1,
             nc.sync.dma_start(out[n * P : (n + 1) * P, cs], res[:, n, cs])
 
         def gate_ln():
-            ends = rate[:].rearrange("p n c -> p (n c)")[:, HALF - 1 : GENE_TILES * S - HALF : HALF]
+            ends = rate[:].rearrange("p n c -> p (n c)")[:, 2 * S + HALF - 1 : GENE_TILES * S - HALF : HALF]
             nc.scalar.activation(one_late[:], ends, ACT.Sign, bias=one_early[:])
 
         nc.vector.memset(table_sc[:].bitcast(I32), 0)
@@ -210,17 +215,21 @@ def tile_list_barcode_log_expression_kernel(tc, tab_words, tab_scales, offs, w1,
         rates(5, 1, 3)
         gate_ln()
         counts(0, 0, 512)
+        counts(1, 0, 512)
         counts(0, 512, 512)
-        counts(1, 0, 1024)
+        counts(1, 512, 512)
         counts(2, 0, 1024)
         counts(3, 0, 1024)
-        counts(4, 0, 1024)
+        counts(4, 0, 512)
+        counts(4, 512, 512)
         counts(5, 0, 512)
         counts(5, 512, 256)
         counts(5, 768, 128)
         counts(5, 896, 128)
-        for n in range(GENE_TILES - 1):
+        for n in range(GENE_TILES - 2):
             finish(n, 0, 1024)
+        finish(4, 0, 512)
+        finish(4, 512, 512)
         finish(5, 0, 512)
         finish(5, 512, 256)
         finish(5, 768, 128)

@@ -160,8 +160,8 @@ def tile_list_barcode_log_expression_kernel(tc, tab_words, tab_scales, offs, w1,
         nc.vector.memset(w4_sc[:].bitcast(I32), 0)
         nc.scalar.activation(one_early[:], zero[:], ACT.Exp)
 
-        nc.sync.dma_start(offsets[:], offs)
         load_w1_part(0, 0, 4, 0, 256)
+        nc.sync.dma_start(offsets[:], offs)
         load_table_sc(nc.sync)
         load_w1_part(0, 0, 4, 256, 256)
         load_table()
@@ -220,8 +220,7 @@ def tile_list_barcode_log_expression_kernel(tc, tab_words, tab_scales, offs, w1,
         counts(1, 512, 512)
         counts(2, 0, 1024)
         counts(3, 0, 1024)
-        counts(4, 0, 512)
-        counts(4, 512, 512)
+        counts(4, 0, 1024)
         counts(5, 0, 512)
         counts(5, 512, 256)
         counts(5, 768, 128)

@@ -35,7 +35,7 @@ def tile_list_barcode_log_expression_kernel(tc, tab_words, tab_scales, offs, w1,
         table = keep.tile([P, T], U32, name="table", align_bytes=64)
         table_sc = keep.tile([P, T], U8, name="table_sc", align_bytes=64)
         w1_raw = [keep.tile([P, PACK, K_PASS], F32, name="w1_raw%d" % b, align_bytes=64) for b in range(PASSES)]
-        w1_bf = [keep.tile([P, PACK * K_PASS], BF16, name="w1_bf%d" % b, align_bytes=64) for b in range(PASSES)]
+        w1_bf = [keep.tile([P, PACK * K_PASS], BF16, name="w1_bf%d" % b, tag="w1_bf%d" % b, align_bytes=64) for b in range(PASSES)]
         w1_q = [keep.tile([P, K_PASS], U32, name="w1_q%d" % b, align_bytes=64) for b in range(PASSES)]
         w1_sc = [keep.tile([P, K_PASS], U8, name="w1_sc%d" % b, align_bytes=64) for b in range(PASSES)]
         w4 = keep.tile([P, PASSES, 2 * N], U8, name="w4", align_bytes=64)
@@ -45,6 +45,7 @@ def tile_list_barcode_log_expression_kernel(tc, tab_words, tab_scales, offs, w1,
         v_sc = keep.tile([P, S], U8, name="v_sc", align_bytes=64)
         h_bf = keep.tile([P, PASSES, S * PACK], BF16, name="h_bf", align_bytes=64)
         h_q = keep.tile([P, PASSES, S], U32, name="h_q", align_bytes=64)
+        late = {}
         h_sc = keep.tile([P, PASSES, S], U8, name="h_sc", align_bytes=64)
         rate = keep.tile([P, GENE_TILES, S], F32, name="rate", align_bytes=64)
         count = keep.tile([P, GENE_TILES, S], F32, name="count", align_bytes=64)
@@ -124,8 +125,15 @@ def tile_list_barcode_log_expression_kernel(tc, tab_words, tab_scales, offs, w1,
             else:
                 nc.vector.tensor_scalar_max(dst, src, 0.0)
 
+        def codes(b, c0, n):
+            if (b, c0) == (0, 0):
+                if "q" not in late:
+                    late.setdefault("q", keep.tile([P, HALF], U32, name="h_q_first", tag="w1_bf1", align_bytes=64))
+                return late["q"][:]
+            return h_q[:, b, cells(c0, n)]
+
         def quant_h(b, c0, n):
-            nc.vector.quantize_mx(h_q[:, b, cells(c0, n)].bitcast(FP8X4), h_sc[:, b, cells(c0, n)],
+            nc.vector.quantize_mx(codes(b, c0, n).bitcast(FP8X4), h_sc[:, b, cells(c0, n)],
                                   h_bf[:, b, cells(c0 * PACK, n * PACK)])
 
         def rate_of(n, c0, w):
@@ -139,7 +147,7 @@ def tile_list_barcode_log_expression_kernel(tc, tab_words, tab_scales, offs, w1,
             for b in range(PASSES):
                 nc.tensor.matmul_mx(acc[:], lhsT=w4[:, b, cells(n * 2 * P, 2 * P)].bitcast(FP4X4),
                                     lhsT_scale=w4_sc[:, b, cells(n * P, P)],
-                                    rhs=h_q[:, b, cs].bitcast(FP8X4), rhs_scale=h_sc[:, b, cs],
+                                    rhs=codes(b, c * HALF, HALF).bitcast(FP8X4), rhs_scale=h_sc[:, b, cs],
                                     start=(b == 0), stop=(b == PASSES - 1))
             nc.scalar.activation(rate_of(n, c * HALF, HALF), acc[:], ACT.Exp)
 
@@ -177,8 +185,7 @@ def tile_list_barcode_log_expression_kernel(tc, tab_words, tab_scales, offs, w1,
         gather_words(0, 256)
         gather_words(256, 256)
         gather_words(512, 512)
-        cast_w1_part(1, 0, 32, "S")
-        cast_w1_part(1, 32, 32, "G")
+        cast_w1_part(1, 0, 64, "G")
         cast_w1_part(1, 64, 64, "V")
         quant_w1(1)
         hidden(0, 0, "S", 0)

@@ -173,8 +173,8 @@ def tile_list_barcode_log_expression_kernel(tc, tab_words, tab_scales, offs, w1,
         load_table_sc(nc.sync)
         load_w1_part(0, 0, 4, 256, 256)
         load_table()
-        load_w1_part(1, 0, 4, 0, 256)
-        load_w1_part(1, 0, 4, 256, 256)
+        load_w1_part(1, 0, 4, 0, 160)
+        load_w1_part(1, 0, 4, 160, 352)
         load_w4()
         for n in range(GENE_TILES):
             nc.sync.dma_start(g[n][:], gT[n * P : (n + 1) * P, :])
@@ -185,8 +185,8 @@ def tile_list_barcode_log_expression_kernel(tc, tab_words, tab_scales, offs, w1,
         gather_words(0, 256)
         gather_words(256, 256)
         gather_words(512, 512)
-        cast_w1_part(1, 0, 64, "G")
-        cast_w1_part(1, 64, 64, "V")
+        cast_w1_part(1, 0, 40, "S")
+        cast_w1_part(1, 40, 88, "V")
         quant_w1(1)
         hidden(0, 0, "S", 0)
         hidden(0, 1, "S", 1)

@@ -174,7 +174,8 @@ def tile_list_barcode_log_expression_kernel(tc, tab_words, tab_scales, offs, w1,
         load_w1_part(0, 0, 4, 256, 256)
         load_table()
         load_w1_part(1, 0, 4, 0, 160)
-        load_w1_part(1, 0, 4, 160, 352)
+        load_w1_part(1, 0, 4, 160, 128)
+        load_w1_part(1, 0, 4, 288, 224)
         load_w4()
         for n in range(GENE_TILES):
             nc.sync.dma_start(g[n][:], gT[n * P : (n + 1) * P, :])
@@ -186,7 +187,8 @@ def tile_list_barcode_log_expression_kernel(tc, tab_words, tab_scales, offs, w1,
         gather_words(256, 256)
         gather_words(512, 512)
         cast_w1_part(1, 0, 40, "S")
-        cast_w1_part(1, 40, 88, "V")
+        cast_w1_part(1, 40, 32, "G")
+        cast_w1_part(1, 72, 56, "V")
         quant_w1(1)
         hidden(0, 0, "S", 0)
         hidden(0, 1, "S", 1)
@@ -199,26 +201,26 @@ def tile_list_barcode_log_expression_kernel(tc, tab_words, tab_scales, offs, w1,
         hidden(1, 0, "V", 7)
         hidden(1, 1, "S", 0)
         hidden(1, 2, "V", 1)
-        hidden(1, 3, "V", 2)
+        hidden(1, 3, "S", 2)
+        hidden(1, 4, "V", 3)
         quant_h(1, 0, 512)
-        hidden(1, 4, "S", 3)
+        hidden(0, 7, "S", 0)
         hidden(1, 5, "S", 4)
-        hidden(0, 7, "S", 1)
         hidden(1, 6, "S", 5)
-        hidden(1, 7, "V", 2)
+        hidden(1, 7, "S", 6)
         quant_h(0, 512, 512)
         quant_h(1, 512, 512)
-        rates(0, 0, 6)
-        rates(1, 0, 7)
-        rates(2, 0, 0)
+        rates(0, 0, 7)
+        rates(1, 0, 1)
+        rates(2, 0, 2)
         rates(3, 0, 3)
-        rates(0, 1, 4)
-        rates(1, 1, 5)
-        rates(2, 1, 1)
-        rates(3, 1, 2)
-        rates(4, 0, 6)
-        rates(4, 1, 7)
-        rates(5, 0, 0)
+        rates(0, 1, 0)
+        rates(1, 1, 4)
+        rates(2, 1, 5)
+        rates(3, 1, 6)
+        rates(4, 0, 7)
+        rates(4, 1, 1)
+        rates(5, 0, 2)
         rates(5, 1, 3)
         gate_ln()
         counts(0, 0, 512)

@@ -21,8 +21,27 @@ PACK = 4
 K_PASS = P * PACK
 PASSES = H // K_PASS
 GENE_TILES = N // P
-HALF = 512
-QUAD = 128
+HALF = S // 2
+GROUP = P
+GROUPS = S // GROUP
+SCALE_ROWS = 4
+LIST_COLUMN = 16
+
+W1_PIECES = (
+    ((256, "scalar"), (256, "scalar")),
+    ((160, "scalar"), (128, "gpsimd"), (224, "vector")),
+)
+WORD_PIECES = (256, 256, 512)
+LAST_PIECES = (512, 256, 128, 128)
+SHARED = GROUP // 2
+
+
+def pieces(widths):
+    return [(sum(widths[:i]), width) for i, width in enumerate(widths)]
+
+
+def span(start, width):
+    return slice(start, start + width)
 
 
 def tile_list_barcode_log_expression_kernel(tc, tab_words, tab_scales, offs, w1, w4_words, w4_scales, gT, out):
@@ -31,214 +50,171 @@ def tile_list_barcode_log_expression_kernel(tc, tab_words, tab_scales, offs, w1,
         keep = ctx.enter_context(tc.tile_pool(name="keep", bufs=1))
         psum = ctx.enter_context(tc.psum_pool(name="psum", bufs=1))
 
-        offsets = keep.tile([P, S // 16], U16, name="offsets")
+        offsets = keep.tile([P, S // LIST_COLUMN], U16, name="offsets")
         table = keep.tile([P, T], U32, name="table", align_bytes=64)
         table_sc = keep.tile([P, T], U8, name="table_sc", align_bytes=64)
-        w1_raw = [keep.tile([P, PACK, K_PASS], F32, name="w1_raw%d" % b, align_bytes=64) for b in range(PASSES)]
-        w1_bf = [keep.tile([P, PACK * K_PASS], BF16, name="w1_bf%d" % b, tag="w1_bf%d" % b, align_bytes=64) for b in range(PASSES)]
-        w1_q = [keep.tile([P, K_PASS], U32, name="w1_q%d" % b, align_bytes=64) for b in range(PASSES)]
-        w1_sc = [keep.tile([P, K_PASS], U8, name="w1_sc%d" % b, align_bytes=64) for b in range(PASSES)]
+        w1_raw = [keep.tile([P, PACK, K_PASS], F32, name="w1_raw%d" % a, align_bytes=64) for a in range(PASSES)]
+        w1_bf = [keep.tile([P, PACK * K_PASS], BF16, name="w1_bf%d" % a, align_bytes=64) for a in range(PASSES)]
+        w1_q = [keep.tile([P, K_PASS], U32, name="w1_q%d" % a, align_bytes=64) for a in range(PASSES)]
+        w1_sc = [keep.tile([P, K_PASS], U8, name="w1_sc%d" % a, align_bytes=64) for a in range(PASSES)]
         w4 = keep.tile([P, PASSES, 2 * N], U8, name="w4", align_bytes=64)
         w4_sc = keep.tile([P, PASSES, N], U8, name="w4_sc", align_bytes=64)
-        g = [keep.tile([P, T], F32, name="g%d" % n, align_bytes=64) for n in range(GENE_TILES)]
+        factors = [keep.tile([P, T], F32, name="factors%d" % n, align_bytes=64) for n in range(GENE_TILES)]
         v_q = keep.tile([P, S], U32, name="v_q", align_bytes=64)
         v_sc = keep.tile([P, S], U8, name="v_sc", align_bytes=64)
         h_bf = keep.tile([P, PASSES, S * PACK], BF16, name="h_bf", align_bytes=64)
         h_q = keep.tile([P, PASSES, S], U32, name="h_q", align_bytes=64)
-        late = {}
         h_sc = keep.tile([P, PASSES, S], U8, name="h_sc", align_bytes=64)
         rate = keep.tile([P, GENE_TILES, S], F32, name="rate", align_bytes=64)
         count = keep.tile([P, GENE_TILES, S], F32, name="count", align_bytes=64)
         res = keep.tile([P, GENE_TILES, S], F32, name="res", align_bytes=64)
         zero = keep.tile([P, 1], F32, name="zero")
         one_early = keep.tile([P, 1], F32, name="one_early")
-        one_late = keep.tile([P, 7], F32, name="one_late")
+        one_late = keep.tile([P, 2 * (GENE_TILES - 2) - 1], F32, name="one_late")
 
-        def cells(c0, n):
-            return slice(c0, c0 + n)
+        def listed(start, width):
+            return offsets[:, start // LIST_COLUMN : (start + width) // LIST_COLUMN]
 
-        def listed(c0, n):
-            return offsets[:, c0 // 16 : (c0 + n) // 16]
+        def load_w1(a, start, width):
+            rows = w1.rearrange("(p j) c -> p j c", j=PACK)
+            nc.sync.dma_start(w1_raw[a][:, :, span(start, width)], rows[:, :, span(a * K_PASS + start, width)])
 
-        def load_w1(b):
-            nc.sync.dma_start(w1_raw[b][:], w1.rearrange("(p j) c -> p j c", j=PACK)[:, :, b * K_PASS : (b + 1) * K_PASS])
-
-        def load_w1_part(b, j0, nj, c0, ncol):
-            src = w1.rearrange("(p j) c -> p j c", j=PACK)
-            nc.sync.dma_start(w1_raw[b][:, j0 : j0 + nj, c0 : c0 + ncol],
-                              src[:, j0 : j0 + nj, b * K_PASS + c0 : b * K_PASS + c0 + ncol])
-
-        def cast_w1_part(b, m0, nm, eng):
-            dst = w1_bf[b][:].rearrange("p (t m j) -> p m j t", t=PACK, j=PACK)[:, m0 : m0 + nm]
-            src = w1_raw[b][:].rearrange("p j (m t) -> p m j t", t=PACK)[:, m0 : m0 + nm]
-            if eng == "S":
+        def round_w1(a, start, width, engine):
+            places = span(start // PACK, width // PACK)
+            dst = w1_bf[a][:].rearrange("p (t m j) -> p m j t", t=PACK, j=PACK)[:, places]
+            src = w1_raw[a][:].rearrange("p j (m t) -> p m j t", t=PACK)[:, places]
+            if engine == "scalar":
                 nc.scalar.copy(dst, src)
-            elif eng == "V":
+            elif engine == "vector":
                 nc.vector.tensor_copy(dst, src)
             else:
-                nc.gpsimd.tensor_scalar(dst.rearrange("p m j t -> p t m j"), src.rearrange("p m j t -> p t m j"), 1.0, 0.0, ALU.mult, ALU.add)
+                nc.gpsimd.tensor_scalar(dst.rearrange("p m j t -> p t m j"), src.rearrange("p m j t -> p t m j"),
+                                        1.0, 0.0, ALU.mult, ALU.add)
 
-        def load_table():
-            nc.sync.dma_start(table[:].bitcast(I32), tab_words[0].rearrange("p t i -> p (t i)").bitcast(I32))
+        def quantise_w1(a):
+            nc.vector.quantize_mx(w1_q[a][:].bitcast(FP8X4), w1_sc[a][:], w1_bf[a][:])
 
-        def load_table_sc(eng):
-            rows = tab_scales[0].rearrange("(q r) t -> r q t", r=4)
-            for r in range(4):
-                eng.dma_start(table_sc[:].bitcast(I32)[r:P:32, :], rows[r].bitcast(I32))
-
-        def load_w4():
-            rows = w4_scales.rearrange("a (q r) c -> r q a c", r=4)
-            for r in range(4):
-                nc.sync.dma_start(w4_sc[:].bitcast(I32)[r:P:32, :, :], rows[r].bitcast(I32))
-            nc.sync.dma_start(w4[:].bitcast(I32), w4_words.rearrange("a p c -> p a c").bitcast(I32))
-
-        def cast_w1(b, eng):
-            dst = w1_bf[b][:].rearrange("p (t m j) -> p m j t", t=PACK, j=PACK)
-            src = w1_raw[b][:].rearrange("p j (m t) -> p m j t", t=PACK)
-            if eng == "S":
-                nc.scalar.copy(dst, src)
-            elif eng == "V":
-                nc.vector.tensor_copy(dst, src)
-            else:
-                nc.gpsimd.tensor_scalar(dst, src, 1.0, 0.0, ALU.mult, ALU.add)
-
-        def quant_w1(b):
-            nc.vector.quantize_mx(w1_q[b][:].bitcast(FP8X4), w1_sc[b][:], w1_bf[b][:])
-
-        def gather_words(c0, n):
-            nc.vector.tensor_copy(v_q[:, cells(c0, n)], table[:].indirect(listed(c0, n)))
-
-        def gather_scales(c0, n):
-            nc.vector.tensor_copy(v_sc[:, cells(c0, n)], table_sc[:].indirect(listed(c0, n)))
-
-        def hidden(b, q, eng, bank):
-            acc = psum.tile([P, PACK, QUAD], F32, name="acc_h", tag="bank%d" % bank)
-            cs = cells(q * QUAD, QUAD)
+        def hidden(a, start, width, engine, bank):
+            acc = psum.tile([P, PACK, width], F32, name="acc_h", tag="bank%d" % bank)
+            cells = span(start, width)
             for t in range(PACK):
-                ms = cells(t * P, P)
-                nc.tensor.matmul_mx(acc[:, t, :], lhsT=w1_q[b][:, ms].bitcast(FP8X4), lhsT_scale=w1_sc[b][:, ms],
-                                    rhs=v_q[:, cs].bitcast(FP8X4), rhs_scale=v_sc[:, cs], start=True, stop=True)
-            dst = h_bf[:, b, cells(q * QUAD * PACK, QUAD * PACK)].rearrange("p (c t) -> p c t", t=PACK)
+                places = span(t * P, P)
+                nc.tensor.matmul_mx(acc[:, t, :], lhsT=w1_q[a][:, places].bitcast(FP8X4), lhsT_scale=w1_sc[a][:, places],
+                                    rhs=v_q[:, cells].bitcast(FP8X4), rhs_scale=v_sc[:, cells], start=True, stop=True)
+            dst = h_bf[:, a, span(start * PACK, width * PACK)].rearrange("p (c t) -> p c t", t=PACK)
             src = acc[:].rearrange("p t c -> p c t")
-            if eng == "S":
+            if engine == "scalar":
                 nc.scalar.activation(dst, src, ACT.Relu)
             else:
                 nc.vector.tensor_scalar_max(dst, src, 0.0)
 
-        def codes(b, c0, n):
-            if (b, c0) == (0, 0):
-                if "q" not in late:
-                    late.setdefault("q", keep.tile([P, HALF], U32, name="h_q_first", tag="w1_bf1", align_bytes=64))
-                return late["q"][:]
-            return h_q[:, b, cells(c0, n)]
+        def hidden_group(a, group, engine, bank):
+            hidden(a, group * GROUP, GROUP, engine, bank)
 
-        def quant_h(b, c0, n):
-            nc.vector.quantize_mx(codes(b, c0, n).bitcast(FP8X4), h_sc[:, b, cells(c0, n)],
-                                  h_bf[:, b, cells(c0 * PACK, n * PACK)])
+        def quantise_h(a, half):
+            cells = span(half * HALF, HALF)
+            nc.vector.quantize_mx(h_q[:, a, cells].bitcast(FP8X4), h_sc[:, a, cells],
+                                  h_bf[:, a, span(half * HALF * PACK, HALF * PACK)])
 
-        def rate_of(n, c0, w):
-            if (n, c0) == (1, 0):
-                return count[:, 0, cells(HALF, HALF)]
-            return rate[:, n, cells(c0, w)]
+        def rate_of(n, start, width):
+            if (n, start) == (1, 0):
+                return count[:, 0, span(HALF, HALF)]
+            return rate[:, n, span(start, width)]
 
-        def rates(n, c, bank):
+        def rates(n, half, bank):
             acc = psum.tile([P, HALF], F32, name="acc_y", tag="bank%d" % bank)
-            cs = cells(c * HALF, HALF)
-            for b in range(PASSES):
-                nc.tensor.matmul_mx(acc[:], lhsT=w4[:, b, cells(n * 2 * P, 2 * P)].bitcast(FP4X4),
-                                    lhsT_scale=w4_sc[:, b, cells(n * P, P)],
-                                    rhs=codes(b, c * HALF, HALF).bitcast(FP8X4), rhs_scale=h_sc[:, b, cs],
-                                    start=(b == 0), stop=(b == PASSES - 1))
-            nc.scalar.activation(rate_of(n, c * HALF, HALF), acc[:], ACT.Exp)
+            cells = span(half * HALF, HALF)
+            for a in range(PASSES):
+                nc.tensor.matmul_mx(acc[:], lhsT=w4[:, a, span(n * 2 * P, 2 * P)].bitcast(FP4X4),
+                                    lhsT_scale=w4_sc[:, a, span(n * P, P)],
+                                    rhs=h_q[:, a, cells].bitcast(FP8X4), rhs_scale=h_sc[:, a, cells],
+                                    start=(a == 0), stop=(a == PASSES - 1))
+            nc.scalar.activation(rate_of(n, half * HALF, HALF), acc[:], ACT.Exp)
 
-        def counts(n, c0, w):
-            nc.vector.tensor_tensor(count[:, n, cells(c0, w)], g[n][:].indirect(listed(c0, w)), rate_of(n, c0, w), ALU.mult)
-
-        def finish(n, c0, w):
-            cs = cells(c0, w)
-            nc.scalar.activation(res[:, n, cs], count[:, n, cs], ACT.Ln, bias=one_late[:, 0:1])
-            nc.sync.dma_start(out[n * P : (n + 1) * P, cs], res[:, n, cs])
-
-        def gate_ln():
+        def hold_logs():
             ends = rate[:].rearrange("p n c -> p (n c)")[:, 2 * S + HALF - 1 : GENE_TILES * S - HALF : HALF]
             nc.scalar.activation(one_late[:], ends, ACT.Sign, bias=one_early[:])
+
+        def counts(n, start, width):
+            nc.vector.tensor_tensor(count[:, n, span(start, width)], factors[n][:].indirect(listed(start, width)),
+                                    rate_of(n, start, width), ALU.mult)
+
+        def finish(n, start, width):
+            cells = span(start, width)
+            nc.scalar.activation(res[:, n, cells], count[:, n, cells], ACT.Ln, bias=one_late[:, 0:1])
+            nc.sync.dma_start(out[span(n * P, P), cells], res[:, n, cells])
 
         nc.vector.memset(table_sc[:].bitcast(I32), 0)
         nc.vector.memset(zero[:], 0.0)
         nc.vector.memset(w4_sc[:].bitcast(I32), 0)
         nc.scalar.activation(one_early[:], zero[:], ACT.Exp)
 
-        load_w1_part(0, 0, 4, 0, 256)
+        w1_pieces = [[(start, width, engine) for (start, width), (width, engine)
+                      in zip(pieces([w for w, e in of_pass]), of_pass)] for of_pass in W1_PIECES]
+        load_w1(0, *w1_pieces[0][0][:2])
         nc.sync.dma_start(offsets[:], offs)
-        load_table_sc(nc.sync)
-        load_w1_part(0, 0, 4, 256, 256)
-        load_table()
-        load_w1_part(1, 0, 4, 0, 160)
-        load_w1_part(1, 0, 4, 160, 128)
-        load_w1_part(1, 0, 4, 288, 224)
-        load_w4()
+        table_rows = tab_scales[0].rearrange("(q r) t -> r q t", r=SCALE_ROWS)
+        for r in range(SCALE_ROWS):
+            nc.sync.dma_start(table_sc[:].bitcast(I32)[r:P:32, :], table_rows[r].bitcast(I32))
+        load_w1(0, *w1_pieces[0][1][:2])
+        nc.sync.dma_start(table[:].bitcast(I32), tab_words[0].rearrange("p t i -> p (t i)").bitcast(I32))
+        for start, width, engine in w1_pieces[1]:
+            load_w1(1, start, width)
+        w4_rows = w4_scales.rearrange("a (q r) c -> r q a c", r=SCALE_ROWS)
+        for r in range(SCALE_ROWS):
+            nc.sync.dma_start(w4_sc[:].bitcast(I32)[r:P:32, :, :], w4_rows[r].bitcast(I32))
+        nc.sync.dma_start(w4[:].bitcast(I32), w4_words.rearrange("a p c -> p a c").bitcast(I32))
         for n in range(GENE_TILES):
-            nc.sync.dma_start(g[n][:], gT[n * P : (n + 1) * P, :])
-        cast_w1_part(0, 0, 64, "S")
-        cast_w1_part(0, 64, 64, "S")
-        gather_scales(0, 1024)
-        quant_w1(0)
-        gather_words(0, 256)
-        gather_words(256, 256)
-        gather_words(512, 512)
-        cast_w1_part(1, 0, 40, "S")
-        cast_w1_part(1, 40, 32, "G")
-        cast_w1_part(1, 72, 56, "V")
-        quant_w1(1)
-        hidden(0, 0, "S", 0)
-        hidden(0, 1, "S", 1)
-        hidden(0, 2, "S", 2)
-        hidden(0, 3, "S", 3)
-        quant_h(0, 0, 512)
-        hidden(0, 4, "S", 4)
-        hidden(0, 5, "S", 5)
-        hidden(0, 6, "S", 6)
-        hidden(1, 0, "V", 7)
-        hidden(1, 1, "S", 0)
-        hidden(1, 2, "V", 1)
-        hidden(1, 3, "S", 2)
-        hidden(1, 4, "V", 3)
-        quant_h(1, 0, 512)
-        hidden(0, 7, "S", 0)
-        hidden(1, 5, "S", 4)
-        hidden(1, 6, "S", 5)
-        hidden(1, 7, "S", 6)
-        quant_h(0, 512, 512)
-        quant_h(1, 512, 512)
-        rates(0, 0, 7)
-        rates(1, 0, 1)
-        rates(2, 0, 2)
-        rates(3, 0, 3)
-        rates(0, 1, 0)
-        rates(1, 1, 4)
-        rates(2, 1, 5)
-        rates(3, 1, 6)
-        rates(4, 0, 7)
-        rates(4, 1, 1)
-        rates(5, 0, 2)
-        rates(5, 1, 3)
-        gate_ln()
-        counts(0, 0, 512)
-        counts(1, 0, 512)
-        counts(0, 512, 512)
-        counts(1, 512, 512)
-        counts(2, 0, 1024)
-        counts(3, 0, 1024)
-        counts(4, 0, 1024)
-        counts(5, 0, 512)
-        counts(5, 512, 256)
-        counts(5, 768, 128)
-        counts(5, 896, 128)
+            nc.sync.dma_start(factors[n][:], gT[span(n * P, P), :])
+
+        for start, width, engine in w1_pieces[0]:
+            round_w1(0, start, width, engine)
+        nc.vector.tensor_copy(v_sc[:], table_sc[:].indirect(listed(0, S)))
+        quantise_w1(0)
+        for start, width in pieces(WORD_PIECES):
+            nc.vector.tensor_copy(v_q[:, span(start, width)], table[:].indirect(listed(start, width)))
+        for start, width, engine in w1_pieces[1]:
+            round_w1(1, start, width, engine)
+        quantise_w1(1)
+
+        last = GROUPS - 1
+        for group in range(GROUPS // 2):
+            hidden_group(0, group, "scalar", group)
+        quantise_h(0, 0)
+        for group in range(GROUPS // 2, last):
+            hidden_group(0, group, "scalar", group)
+        for group in range(GROUPS // 2 + 1):
+            hidden_group(1, group, "scalar" if group % 2 else "vector", (group - 1) % GROUPS)
+        quantise_h(1, 0)
+        hidden_group(0, last, "scalar", 0)
+        hidden_group(1, last - 2, "scalar", 4)
+        hidden(1, (last - 1) * GROUP, SHARED, "vector", 5)
+        hidden(1, (last - 1) * GROUP + SHARED, GROUP - SHARED, "scalar", 7)
+        hidden_group(1, last, "scalar", 6)
+        quantise_h(0, 1)
+        quantise_h(1, 1)
+
+        early = range(4)
+        for n, bank in zip(early, (1, 2, 3, 0)):
+            rates(n, 0, bank)
+        for n, bank in zip(early, (5, 4, 7, 6)):
+            rates(n, 1, bank)
+        for n, banks in zip(range(len(early), GENE_TILES), ((1, 2), (3, 0))):
+            for half in range(2):
+                rates(n, half, banks[half])
+        hold_logs()
+
+        for half in range(2):
+            for n in range(2):
+                counts(n, half * HALF, HALF)
+        for n in range(2, GENE_TILES - 1):
+            counts(n, 0, S)
+        for start, width in pieces(LAST_PIECES):
+            counts(GENE_TILES - 1, start, width)
+
         for n in range(GENE_TILES - 2):
-            finish(n, 0, 1024)
-        finish(4, 0, 512)
-        finish(4, 512, 512)
-        finish(5, 0, 512)
-        finish(5, 512, 256)
-        finish(5, 768, 128)
-        finish(5, 896, 128)
+            finish(n, 0, S)
+        for half in range(2):
+            finish(GENE_TILES - 2, half * HALF, HALF)
+        for start, width in pieces(LAST_PIECES):
+            finish(GENE_TILES - 1, start, width)

@@ -23,7 +23,6 @@ PASSES = H // K_PASS
 GENE_TILES = N // P
 HALF = S // 2
 GROUP = P
-GROUPS = S // GROUP
 SCALE_ROWS = 4
 LIST_COLUMN = 16
 
@@ -34,6 +33,7 @@ W1_PIECES = (
 WORD_PIECES = (256, 256, 512)
 LAST_PIECES = (512, 256, 128, 128)
 SHARED = GROUP // 2
+H_TAGS = (("w1_raw1_0", "h_bf01"), ("h_bf10", "h_bf11"))
 
 
 def pieces(widths):
@@ -53,7 +53,10 @@ def tile_list_barcode_log_expression_kernel(tc, tab_words, tab_scales, offs, w1,
         offsets = keep.tile([P, S // LIST_COLUMN], U16, name="offsets")
         table = keep.tile([P, T], U32, name="table", align_bytes=64)
         table_sc = keep.tile([P, T], U8, name="table_sc", align_bytes=64)
-        w1_raw = [keep.tile([P, PACK, K_PASS], F32, name="w1_raw%d" % a, align_bytes=64) for a in range(PASSES)]
+        w1_pieces = [[(start, width, engine) for (start, width), (width, engine)
+                      in zip(pieces([w for w, e in of_pass]), of_pass)] for of_pass in W1_PIECES]
+        w1_raw = {(a, start): keep.tile([P, PACK, width], F32, name="w1_raw%d_%d" % (a, start), align_bytes=64)
+                  for a in range(PASSES) for start, width, engine in w1_pieces[a]}
         w1_bf = [keep.tile([P, PACK * K_PASS], BF16, name="w1_bf%d" % a, align_bytes=64) for a in range(PASSES)]
         w1_q = [keep.tile([P, K_PASS], U32, name="w1_q%d" % a, align_bytes=64) for a in range(PASSES)]
         w1_sc = [keep.tile([P, K_PASS], U8, name="w1_sc%d" % a, align_bytes=64) for a in range(PASSES)]
@@ -62,7 +65,7 @@ def tile_list_barcode_log_expression_kernel(tc, tab_words, tab_scales, offs, w1,
         factors = [keep.tile([P, T], F32, name="factors%d" % n, align_bytes=64) for n in range(GENE_TILES)]
         v_q = keep.tile([P, S], U32, name="v_q", align_bytes=64)
         v_sc = keep.tile([P, S], U8, name="v_sc", align_bytes=64)
-        h_bf = keep.tile([P, PASSES, S * PACK], BF16, name="h_bf", align_bytes=64)
+        h_bf = {}
         h_q = keep.tile([P, PASSES, S], U32, name="h_q", align_bytes=64)
         h_sc = keep.tile([P, PASSES, S], U8, name="h_sc", align_bytes=64)
         rate = keep.tile([P, GENE_TILES, S], F32, name="rate", align_bytes=64)
@@ -77,12 +80,12 @@ def tile_list_barcode_log_expression_kernel(tc, tab_words, tab_scales, offs, w1,
 
         def load_w1(a, start, width):
             rows = w1.rearrange("(p j) c -> p j c", j=PACK)
-            nc.sync.dma_start(w1_raw[a][:, :, span(start, width)], rows[:, :, span(a * K_PASS + start, width)])
+            nc.sync.dma_start(w1_raw[a, start][:], rows[:, :, span(a * K_PASS + start, width)])
 
         def round_w1(a, start, width, engine):
             places = span(start // PACK, width // PACK)
             dst = w1_bf[a][:].rearrange("p (t m j) -> p m j t", t=PACK, j=PACK)[:, places]
-            src = w1_raw[a][:].rearrange("p j (m t) -> p m j t", t=PACK)[:, places]
+            src = w1_raw[a, start][:].rearrange("p j (m t) -> p m j t", t=PACK)
             if engine == "scalar":
                 nc.scalar.copy(dst, src)
             elif engine == "vector":
@@ -101,7 +104,11 @@ def tile_list_barcode_log_expression_kernel(tc, tab_words, tab_scales, offs, w1,
                 places = span(t * P, P)
                 nc.tensor.matmul_mx(acc[:, t, :], lhsT=w1_q[a][:, places].bitcast(FP8X4), lhsT_scale=w1_sc[a][:, places],
                                     rhs=v_q[:, cells].bitcast(FP8X4), rhs_scale=v_sc[:, cells], start=True, stop=True)
-            dst = h_bf[:, a, span(start * PACK, width * PACK)].rearrange("p (c t) -> p c t", t=PACK)
+            half = start // HALF
+            if (a, half) not in h_bf:
+                h_bf.setdefault((a, half), keep.tile([P, HALF * PACK], BF16, name="h_bf", align_bytes=64,
+                                                     tag=H_TAGS[a][half]))
+            dst = h_bf[a, half][:, span((start - half * HALF) * PACK, width * PACK)].rearrange("p (c t) -> p c t", t=PACK)
             src = acc[:].rearrange("p t c -> p c t")
             if engine == "scalar":
                 nc.scalar.activation(dst, src, ACT.Relu)
@@ -114,7 +121,7 @@ def tile_list_barcode_log_expression_kernel(tc, tab_words, tab_scales, offs, w1,
         def quantise_h(a, half):
             cells = span(half * HALF, HALF)
             nc.vector.quantize_mx(h_q[:, a, cells].bitcast(FP8X4), h_sc[:, a, cells],
-                                  h_bf[:, a, span(half * HALF * PACK, HALF * PACK)])
+                                  h_bf[a, half][:])
 
         def rate_of(n, start, width):
             if (n, start) == (1, 0):
@@ -149,8 +156,6 @@ def tile_list_barcode_log_expression_kernel(tc, tab_words, tab_scales, offs, w1,
         nc.vector.memset(w4_sc[:].bitcast(I32), 0)
         nc.scalar.activation(one_early[:], zero[:], ACT.Exp)
 
-        w1_pieces = [[(start, width, engine) for (start, width), (width, engine)
-                      in zip(pieces([w for w, e in of_pass]), of_pass)] for of_pass in W1_PIECES]
         load_w1(0, *w1_pieces[0][0][:2])
         nc.sync.dma_start(offsets[:], offs)
         table_rows = tab_scales[0].rearrange("(q r) t -> r q t", r=SCALE_ROWS)
@@ -177,29 +182,28 @@ def tile_list_barcode_log_expression_kernel(tc, tab_words, tab_scales, offs, w1,
             round_w1(1, start, width, engine)
         quantise_w1(1)
 
-        last = GROUPS - 1
-        for group in range(GROUPS // 2):
+        for group in range(4):
             hidden_group(0, group, "scalar", group)
         quantise_h(0, 0)
-        for group in range(GROUPS // 2, last):
+        for group in range(4, 7):
             hidden_group(0, group, "scalar", group)
-        for group in range(GROUPS // 2 + 1):
-            hidden_group(1, group, "scalar" if group % 2 else "vector", (group - 1) % GROUPS)
+        for group, bank in zip(range(3), (7, 0, 1)):
+            hidden_group(1, group, "vector", bank)
+        hidden_group(1, 3, "scalar", 2)
+        hidden_group(1, 4, "vector", 3)
         quantise_h(1, 0)
-        hidden_group(0, last, "scalar", 0)
-        hidden_group(1, last - 2, "scalar", 4)
-        hidden(1, (last - 1) * GROUP, SHARED, "vector", 5)
-        hidden(1, (last - 1) * GROUP + SHARED, GROUP - SHARED, "scalar", 7)
-        hidden_group(1, last, "scalar", 6)
+        hidden_group(1, 5, "scalar", 4)
+        hidden_group(0, 7, "scalar", 2)
+        hidden_group(1, 6, "scalar", 5)
+        hidden_group(1, 7, "scalar", 6)
         quantise_h(0, 1)
         quantise_h(1, 1)
 
-        early = range(4)
-        for n, bank in zip(early, (1, 2, 3, 0)):
+        for n, bank in zip(range(4), (7, 0, 1, 3)):
             rates(n, 0, bank)
-        for n, bank in zip(early, (5, 4, 7, 6)):
+        for n, bank in zip(range(4), (4, 2, 5, 6)):
             rates(n, 1, bank)
-        for n, banks in zip(range(len(early), GENE_TILES), ((1, 2), (3, 0))):
+        for n, banks in zip(range(4, GENE_TILES), ((1, 3), (4, 2))):
             for half in range(2):
                 rates(n, half, banks[half])
         hold_logs()

@@ -26,14 +26,15 @@ GROUP = P
 SCALE_ROWS = 4
 LIST_COLUMN = 16
 
-W1_PIECES = (
-    ((256, "scalar"), (256, "scalar")),
-    ((160, "scalar"), (128, "gpsimd"), (224, "vector")),
+W1_LOADS = ((128, 384), (160, 128, 224))
+W1_ROUNDS = (
+    (((128, "scalar"),), ((192, "scalar"), (192, "vector"))),
+    (((160, "scalar"),), ((128, "gpsimd"),), ((224, "vector"),)),
 )
 WORD_PIECES = (256, 256, 512)
 LAST_PIECES = (512, 256, 128, 128)
 SHARED = GROUP // 2
-H_TAGS = (("w1_raw1_0", "h_bf01"), ("h_bf10", "h_bf11"))
+H_TAGS = (("h_bf00", "h_bf01"), ("h_bf10", "h_bf11"))
 
 
 def pieces(widths):
@@ -53,10 +54,9 @@ def tile_list_barcode_log_expression_kernel(tc, tab_words, tab_scales, offs, w1,
         offsets = keep.tile([P, S // LIST_COLUMN], U16, name="offsets")
         table = keep.tile([P, T], U32, name="table", align_bytes=64)
         table_sc = keep.tile([P, T], U8, name="table_sc", align_bytes=64)
-        w1_pieces = [[(start, width, engine) for (start, width), (width, engine)
-                      in zip(pieces([w for w, e in of_pass]), of_pass)] for of_pass in W1_PIECES]
+        w1_pieces = [pieces(widths) for widths in W1_LOADS]
         w1_raw = {(a, start): keep.tile([P, PACK, width], F32, name="w1_raw%d_%d" % (a, start), align_bytes=64)
-                  for a in range(PASSES) for start, width, engine in w1_pieces[a]}
+                  for a in range(PASSES) for start, width in w1_pieces[a]}
         w1_bf = [keep.tile([P, PACK * K_PASS], BF16, name="w1_bf%d" % a, align_bytes=64) for a in range(PASSES)]
         w1_q = [keep.tile([P, K_PASS], U32, name="w1_q%d" % a, align_bytes=64) for a in range(PASSES)]
         w1_sc = [keep.tile([P, K_PASS], U8, name="w1_sc%d" % a, align_bytes=64) for a in range(PASSES)]
@@ -82,10 +82,15 @@ def tile_list_barcode_log_expression_kernel(tc, tab_words, tab_scales, offs, w1,
             rows = w1.rearrange("(p j) c -> p j c", j=PACK)
             nc.sync.dma_start(w1_raw[a, start][:], rows[:, :, span(a * K_PASS + start, width)])
 
-        def round_w1(a, start, width, engine):
-            places = span(start // PACK, width // PACK)
+        def round_w1(a):
+            for (first, loaded), shares in zip(w1_pieces[a], W1_ROUNDS[a]):
+                for (skip, width), (width, engine) in zip(pieces([w for w, e in shares]), shares):
+                    round_share(a, first, skip, width, engine)
+
+        def round_share(a, first, skip, width, engine):
+            places = span((first + skip) // PACK, width // PACK)
             dst = w1_bf[a][:].rearrange("p (t m j) -> p m j t", t=PACK, j=PACK)[:, places]
-            src = w1_raw[a, start][:].rearrange("p j (m t) -> p m j t", t=PACK)
+            src = w1_raw[a, first][:].rearrange("p j (m t) -> p m j t", t=PACK)[:, span(skip // PACK, width // PACK)]
             if engine == "scalar":
                 nc.scalar.copy(dst, src)
             elif engine == "vector":
@@ -151,19 +156,20 @@ def tile_list_barcode_log_expression_kernel(tc, tab_words, tab_scales, offs, w1,
             nc.scalar.activation(res[:, n, cells], count[:, n, cells], ACT.Ln, bias=one_late[:, 0:1])
             nc.sync.dma_start(out[span(n * P, P), cells], res[:, n, cells])
 
-        nc.vector.memset(table_sc[:].bitcast(I32), 0)
+        nc.vector.memset(table_sc[:, : T // 2].bitcast(I32), 0)
+        nc.gpsimd.memset(table_sc[:, T // 2 :].bitcast(I32), 0)
         nc.vector.memset(zero[:], 0.0)
         nc.vector.memset(w4_sc[:].bitcast(I32), 0)
         nc.scalar.activation(one_early[:], zero[:], ACT.Exp)
 
-        load_w1(0, *w1_pieces[0][0][:2])
+        load_w1(0, *w1_pieces[0][0])
         nc.sync.dma_start(offsets[:], offs)
         table_rows = tab_scales[0].rearrange("(q r) t -> r q t", r=SCALE_ROWS)
         for r in range(SCALE_ROWS):
             nc.sync.dma_start(table_sc[:].bitcast(I32)[r:P:32, :], table_rows[r].bitcast(I32))
-        load_w1(0, *w1_pieces[0][1][:2])
+        load_w1(0, *w1_pieces[0][1])
         nc.sync.dma_start(table[:].bitcast(I32), tab_words[0].rearrange("p t i -> p (t i)").bitcast(I32))
-        for start, width, engine in w1_pieces[1]:
+        for start, width in w1_pieces[1]:
             load_w1(1, start, width)
         w4_rows = w4_scales.rearrange("a (q r) c -> r q a c", r=SCALE_ROWS)
         for r in range(SCALE_ROWS):
@@ -172,14 +178,12 @@ def tile_list_barcode_log_expression_kernel(tc, tab_words, tab_scales, offs, w1,
         for n in range(GENE_TILES):
             nc.sync.dma_start(factors[n][:], gT[span(n * P, P), :])
 
-        for start, width, engine in w1_pieces[0]:
-            round_w1(0, start, width, engine)
         nc.vector.tensor_copy(v_sc[:], table_sc[:].indirect(listed(0, S)))
+        round_w1(0)
         quantise_w1(0)
         for start, width in pieces(WORD_PIECES):
             nc.vector.tensor_copy(v_q[:, span(start, width)], table[:].indirect(listed(start, width)))
-        for start, width, engine in w1_pieces[1]:
-            round_w1(1, start, width, engine)
+        round_w1(1)
         quantise_w1(1)
 
         for group in range(4):
@@ -187,23 +191,22 @@ def tile_list_barcode_log_expression_kernel(tc, tab_words, tab_scales, offs, w1,
         quantise_h(0, 0)
         for group in range(4, 7):
             hidden_group(0, group, "scalar", group)
-        for group, bank in zip(range(3), (7, 0, 1)):
-            hidden_group(1, group, "vector", bank)
-        hidden_group(1, 3, "scalar", 2)
-        hidden_group(1, 4, "vector", 3)
+        for group in range(5):
+            hidden_group(1, group, "scalar" if group % 2 else "vector", (group - 1) % 8)
         quantise_h(1, 0)
+        hidden_group(0, 7, "scalar", 0)
         hidden_group(1, 5, "scalar", 4)
-        hidden_group(0, 7, "scalar", 2)
-        hidden_group(1, 6, "scalar", 5)
+        hidden(1, 6 * GROUP, SHARED, "vector", 5)
+        hidden(1, 6 * GROUP + SHARED, GROUP - SHARED, "scalar", 7)
         hidden_group(1, 7, "scalar", 6)
         quantise_h(0, 1)
         quantise_h(1, 1)
 
-        for n, bank in zip(range(4), (7, 0, 1, 3)):
+        for n, bank in zip(range(4), (1, 2, 3, 0)):
             rates(n, 0, bank)
-        for n, bank in zip(range(4), (4, 2, 5, 6)):
+        for n, bank in zip(range(4), (5, 4, 7, 6)):
             rates(n, 1, bank)
-        for n, banks in zip(range(4, GENE_TILES), ((1, 3), (4, 2))):
+        for n, banks in zip(range(4, GENE_TILES), ((1, 2), (3, 0))):
             for half in range(2):
                 rates(n, half, banks[half])
         hold_logs()

@@ -26,9 +26,9 @@ GROUP = P
 SCALE_ROWS = 4
 LIST_COLUMN = 16
 
-W1_LOADS = ((128, 384), (160, 128, 224))
+W1_LOADS = ((256, 256), (160, 128, 224))
 W1_ROUNDS = (
-    (((128, "scalar"),), ((192, "scalar"), (192, "vector"))),
+    (((256, "scalar"),), ((256, "scalar"),)),
     (((160, "scalar"),), ((128, "gpsimd"),), ((224, "vector"),)),
 )
 WORD_PIECES = (256, 256, 512)
@@ -156,8 +156,7 @@ def tile_list_barcode_log_expression_kernel(tc, tab_words, tab_scales, offs, w1,
             nc.scalar.activation(res[:, n, cells], count[:, n, cells], ACT.Ln, bias=one_late[:, 0:1])
             nc.sync.dma_start(out[span(n * P, P), cells], res[:, n, cells])
 
-        nc.vector.memset(table_sc[:, : T // 2].bitcast(I32), 0)
-        nc.gpsimd.memset(table_sc[:, T // 2 :].bitcast(I32), 0)
+        nc.vector.memset(table_sc[:].bitcast(I32), 0)
         nc.vector.memset(zero[:], 0.0)
         nc.vector.memset(w4_sc[:].bitcast(I32), 0)
         nc.scalar.activation(one_early[:], zero[:], ACT.Exp)
@@ -194,19 +193,19 @@ def tile_list_barcode_log_expression_kernel(tc, tab_words, tab_scales, offs, w1,
         for group in range(5):
             hidden_group(1, group, "scalar" if group % 2 else "vector", (group - 1) % 8)
         quantise_h(1, 0)
-        hidden_group(0, 7, "scalar", 0)
-        hidden_group(1, 5, "scalar", 4)
-        hidden(1, 6 * GROUP, SHARED, "vector", 5)
-        hidden(1, 6 * GROUP + SHARED, GROUP - SHARED, "scalar", 7)
-        hidden_group(1, 7, "scalar", 6)
+        hidden_group(0, 7, "scalar", 4)
+        hidden_group(1, 5, "scalar", 5)
+        hidden(1, 6 * GROUP, SHARED, "vector", 7)
+        hidden(1, 6 * GROUP + SHARED, GROUP - SHARED, "scalar", 6)
+        hidden_group(1, 7, "scalar", 0)
         quantise_h(0, 1)
         quantise_h(1, 1)
 
-        for n, bank in zip(range(4), (1, 2, 3, 0)):
+        for n, bank in zip(range(4), (1, 2, 3, 4)):
             rates(n, 0, bank)
-        for n, bank in zip(range(4), (5, 4, 7, 6)):
+        for n, bank in zip(range(4), (5, 7, 6, 0)):
             rates(n, 1, bank)
-        for n, banks in zip(range(4, GENE_TILES), ((1, 2), (3, 0))):
+        for n, banks in zip(range(4, GENE_TILES), ((1, 2), (3, 4))):
             for half in range(2):
                 rates(n, half, banks[half])
         hold_logs()

@@ -133,14 +133,25 @@ def tile_list_barcode_log_expression_kernel(tc, tab_words, tab_scales, offs, w1,
                 return count[:, 0, span(HALF, HALF)]
             return rate[:, n, span(start, width)]
 
-        def rates(n, half, bank):
-            acc = psum.tile([P, HALF], F32, name="acc_y", tag="bank%d" % bank)
+        opened = {}
+
+        def log_rate_pass(acc, n, half, a):
             cells = span(half * HALF, HALF)
-            for a in range(PASSES):
-                nc.tensor.matmul_mx(acc[:], lhsT=w4[:, a, span(n * 2 * P, 2 * P)].bitcast(FP4X4),
-                                    lhsT_scale=w4_sc[:, a, span(n * P, P)],
-                                    rhs=h_q[:, a, cells].bitcast(FP8X4), rhs_scale=h_sc[:, a, cells],
-                                    start=(a == 0), stop=(a == PASSES - 1))
+            nc.tensor.matmul_mx(acc[:], lhsT=w4[:, a, span(n * 2 * P, 2 * P)].bitcast(FP4X4),
+                                lhsT_scale=w4_sc[:, a, span(n * P, P)],
+                                rhs=h_q[:, a, cells].bitcast(FP8X4), rhs_scale=h_sc[:, a, cells],
+                                start=(a == 0), stop=(a == PASSES - 1))
+
+        def open_rates(n, half, bank):
+            acc = psum.tile([P, HALF], F32, name="acc_y", tag="bank%d" % bank)
+            opened.setdefault((n, half), acc)
+            log_rate_pass(acc, n, half, 0)
+
+        def rates(n, half, bank):
+            if (n, half) not in opened:
+                open_rates(n, half, bank)
+            acc = opened[n, half]
+            log_rate_pass(acc, n, half, 1)
             nc.scalar.activation(rate_of(n, half * HALF, HALF), acc[:], ACT.Exp)
 
         def hold_logs():
@@ -195,17 +206,20 @@ def tile_list_barcode_log_expression_kernel(tc, tab_words, tab_scales, offs, w1,
         quantise_h(1, 0)
         hidden_group(0, 7, "scalar", 4)
         hidden_group(1, 5, "scalar", 5)
-        hidden(1, 6 * GROUP, SHARED, "vector", 7)
-        hidden(1, 6 * GROUP + SHARED, GROUP - SHARED, "scalar", 6)
-        hidden_group(1, 7, "scalar", 0)
+        hidden_group(1, 6, "vector", 7)
+        hidden_group(1, 7, "scalar", 6)
+        for n, bank in zip(range(3), (1, 0, 3)):
+            open_rates(n, 0, bank)
         quantise_h(0, 1)
         quantise_h(1, 1)
 
-        for n, bank in zip(range(4), (1, 2, 3, 4)):
+        for n, bank in zip(range(4), (1, 0, 3, 2)):
             rates(n, 0, bank)
-        for n, bank in zip(range(4), (5, 7, 6, 0)):
+        for n, bank in zip(range(2), (4, 5)):
+            open_rates(n, 1, bank)
+        for n, bank in zip(range(4), (4, 5, 7, 6)):
             rates(n, 1, bank)
-        for n, banks in zip(range(4, GENE_TILES), ((1, 2), (3, 4))):
+        for n, banks in zip(range(4, GENE_TILES), ((1, 0), (3, 2))):
             for half in range(2):
                 rates(n, half, banks[half])
         hold_logs()

@@ -26,15 +26,13 @@ GROUP = P
 SCALE_ROWS = 4
 LIST_COLUMN = 16
 
-W1_LOADS = ((256, 256), (160, 128, 224))
-W1_ROUNDS = (
-    (((256, "scalar"),), ((256, "scalar"),)),
-    (((160, "scalar"),), ((128, "gpsimd"),), ((224, "vector"),)),
+W1_PIECES = (
+    ((256, "scalar"), (256, "scalar")),
+    ((160, "scalar"), (128, "gpsimd"), (224, "vector")),
 )
 WORD_PIECES = (256, 256, 512)
 LAST_PIECES = (512, 256, 128, 128)
 SHARED = GROUP // 2
-H_TAGS = (("h_bf00", "h_bf01"), ("h_bf10", "h_bf11"))
 
 
 def pieces(widths):
@@ -54,9 +52,7 @@ def tile_list_barcode_log_expression_kernel(tc, tab_words, tab_scales, offs, w1,
         offsets = keep.tile([P, S // LIST_COLUMN], U16, name="offsets")
         table = keep.tile([P, T], U32, name="table", align_bytes=64)
         table_sc = keep.tile([P, T], U8, name="table_sc", align_bytes=64)
-        w1_pieces = [pieces(widths) for widths in W1_LOADS]
-        w1_raw = {(a, start): keep.tile([P, PACK, width], F32, name="w1_raw%d_%d" % (a, start), align_bytes=64)
-                  for a in range(PASSES) for start, width in w1_pieces[a]}
+        w1_raw = [keep.tile([P, PACK, K_PASS], F32, name="w1_raw%d" % a, align_bytes=64) for a in range(PASSES)]
         w1_bf = [keep.tile([P, PACK * K_PASS], BF16, name="w1_bf%d" % a, align_bytes=64) for a in range(PASSES)]
         w1_q = [keep.tile([P, K_PASS], U32, name="w1_q%d" % a, align_bytes=64) for a in range(PASSES)]
         w1_sc = [keep.tile([P, K_PASS], U8, name="w1_sc%d" % a, align_bytes=64) for a in range(PASSES)]
@@ -65,7 +61,7 @@ def tile_list_barcode_log_expression_kernel(tc, tab_words, tab_scales, offs, w1,
         factors = [keep.tile([P, T], F32, name="factors%d" % n, align_bytes=64) for n in range(GENE_TILES)]
         v_q = keep.tile([P, S], U32, name="v_q", align_bytes=64)
         v_sc = keep.tile([P, S], U8, name="v_sc", align_bytes=64)
-        h_bf = {}
+        h_bf = keep.tile([P, PASSES, S * PACK], BF16, name="h_bf", align_bytes=64)
         h_q = keep.tile([P, PASSES, S], U32, name="h_q", align_bytes=64)
         h_sc = keep.tile([P, PASSES, S], U8, name="h_sc", align_bytes=64)
         rate = keep.tile([P, GENE_TILES, S], F32, name="rate", align_bytes=64)
@@ -80,17 +76,12 @@ def tile_list_barcode_log_expression_kernel(tc, tab_words, tab_scales, offs, w1,
 
         def load_w1(a, start, width):
             rows = w1.rearrange("(p j) c -> p j c", j=PACK)
-            nc.sync.dma_start(w1_raw[a, start][:], rows[:, :, span(a * K_PASS + start, width)])
+            nc.sync.dma_start(w1_raw[a][:, :, span(start, width)], rows[:, :, span(a * K_PASS + start, width)])
 
-        def round_w1(a):
-            for (first, loaded), shares in zip(w1_pieces[a], W1_ROUNDS[a]):
-                for (skip, width), (width, engine) in zip(pieces([w for w, e in shares]), shares):
-                    round_share(a, first, skip, width, engine)
-
-        def round_share(a, first, skip, width, engine):
-            places = span((first + skip) // PACK, width // PACK)
+        def round_w1(a, start, width, engine):
+            places = span(start // PACK, width // PACK)
             dst = w1_bf[a][:].rearrange("p (t m j) -> p m j t", t=PACK, j=PACK)[:, places]
-            src = w1_raw[a, first][:].rearrange("p j (m t) -> p m j t", t=PACK)[:, span(skip // PACK, width // PACK)]
+            src = w1_raw[a][:].rearrange("p j (m t) -> p m j t", t=PACK)[:, places]
             if engine == "scalar":
                 nc.scalar.copy(dst, src)
             elif engine == "vector":
@@ -109,11 +100,7 @@ def tile_list_barcode_log_expression_kernel(tc, tab_words, tab_scales, offs, w1,
                 places = span(t * P, P)
                 nc.tensor.matmul_mx(acc[:, t, :], lhsT=w1_q[a][:, places].bitcast(FP8X4), lhsT_scale=w1_sc[a][:, places],
                                     rhs=v_q[:, cells].bitcast(FP8X4), rhs_scale=v_sc[:, cells], start=True, stop=True)
-            half = start // HALF
-            if (a, half) not in h_bf:
-                h_bf.setdefault((a, half), keep.tile([P, HALF * PACK], BF16, name="h_bf", align_bytes=64,
-                                                     tag=H_TAGS[a][half]))
-            dst = h_bf[a, half][:, span((start - half * HALF) * PACK, width * PACK)].rearrange("p (c t) -> p c t", t=PACK)
+            dst = h_bf[:, a, span(start * PACK, width * PACK)].rearrange("p (c t) -> p c t", t=PACK)
             src = acc[:].rearrange("p t c -> p c t")
             if engine == "scalar":
                 nc.scalar.activation(dst, src, ACT.Relu)
@@ -126,7 +113,7 @@ def tile_list_barcode_log_expression_kernel(tc, tab_words, tab_scales, offs, w1,
         def quantise_h(a, half):
             cells = span(half * HALF, HALF)
             nc.vector.quantize_mx(h_q[:, a, cells].bitcast(FP8X4), h_sc[:, a, cells],
-                                  h_bf[a, half][:])
+                                  h_bf[:, a, span(half * HALF * PACK, HALF * PACK)])
 
         def rate_of(n, start, width):
             if (n, start) == (1, 0):
@@ -172,14 +159,16 @@ def tile_list_barcode_log_expression_kernel(tc, tab_words, tab_scales, offs, w1,
         nc.vector.memset(w4_sc[:].bitcast(I32), 0)
         nc.scalar.activation(one_early[:], zero[:], ACT.Exp)
 
-        load_w1(0, *w1_pieces[0][0])
+        w1_pieces = [[(start, width, engine) for (start, width), (width, engine)
+                      in zip(pieces([w for w, e in of_pass]), of_pass)] for of_pass in W1_PIECES]
+        load_w1(0, *w1_pieces[0][0][:2])
         nc.sync.dma_start(offsets[:], offs)
         table_rows = tab_scales[0].rearrange("(q r) t -> r q t", r=SCALE_ROWS)
         for r in range(SCALE_ROWS):
             nc.sync.dma_start(table_sc[:].bitcast(I32)[r:P:32, :], table_rows[r].bitcast(I32))
-        load_w1(0, *w1_pieces[0][1])
+        load_w1(0, *w1_pieces[0][1][:2])
         nc.sync.dma_start(table[:].bitcast(I32), tab_words[0].rearrange("p t i -> p (t i)").bitcast(I32))
-        for start, width in w1_pieces[1]:
+        for start, width, engine in w1_pieces[1]:
             load_w1(1, start, width)
         w4_rows = w4_scales.rearrange("a (q r) c -> r q a c", r=SCALE_ROWS)
         for r in range(SCALE_ROWS):
@@ -188,12 +177,14 @@ def tile_list_barcode_log_expression_kernel(tc, tab_words, tab_scales, offs, w1,
         for n in range(GENE_TILES):
             nc.sync.dma_start(factors[n][:], gT[span(n * P, P), :])
 
+        for start, width, engine in w1_pieces[0]:
+            round_w1(0, start, width, engine)
         nc.vector.tensor_copy(v_sc[:], table_sc[:].indirect(listed(0, S)))
-        round_w1(0)
         quantise_w1(0)
         for start, width in pieces(WORD_PIECES):
             nc.vector.tensor_copy(v_q[:, span(start, width)], table[:].indirect(listed(start, width)))
-        round_w1(1)
+        for start, width, engine in w1_pieces[1]:
+            round_w1(1, start, width, engine)
         quantise_w1(1)
 
         for group in range(4):
@@ -213,6 +204,7 @@ def tile_list_barcode_log_expression_kernel(tc, tab_words, tab_scales, offs, w1,
         quantise_h(0, 1)
         quantise_h(1, 1)
 
+
         for n, bank in zip(range(4), (1, 0, 3, 2)):
             rates(n, 0, bank)
         for n, bank in zip(range(2), (4, 5)):
@@ -223,6 +215,7 @@ def tile_list_barcode_log_expression_kernel(tc, tab_words, tab_scales, offs, w1,
             for half in range(2):
                 rates(n, half, banks[half])
         hold_logs()
+
 
         for half in range(2):
             for n in range(2):

@@ -28,10 +28,10 @@ LIST_COLUMN = 16
 
 W1_PIECES = (
     ((256, "scalar"), (256, "scalar")),
-    ((160, "scalar"), (128, "gpsimd"), (224, "vector")),
+    ((128, "scalar"), (192, "gpsimd"), (192, "vector")),
 )
 WORD_PIECES = (256, 256, 512)
-LAST_PIECES = (512, 256, 128, 128)
+LAST_PIECES = (512, 256, 192, 64)
 SHARED = GROUP // 2
 
 
@@ -50,23 +50,23 @@ def tile_list_barcode_log_expression_kernel(tc, tab_words, tab_scales, offs, w1,
         psum = ctx.enter_context(tc.psum_pool(name="psum", bufs=1))
 
         offsets = keep.tile([P, S // LIST_COLUMN], U16, name="offsets")
-        table = keep.tile([P, T], U32, name="table", align_bytes=64)
-        table_sc = keep.tile([P, T], U8, name="table_sc", align_bytes=64)
-        w1_raw = [keep.tile([P, PACK, K_PASS], F32, name="w1_raw%d" % a, align_bytes=64) for a in range(PASSES)]
-        w1_bf = [keep.tile([P, PACK * K_PASS], BF16, name="w1_bf%d" % a, align_bytes=64) for a in range(PASSES)]
-        w1_q = [keep.tile([P, K_PASS], U32, name="w1_q%d" % a, align_bytes=64) for a in range(PASSES)]
-        w1_sc = [keep.tile([P, K_PASS], U8, name="w1_sc%d" % a, align_bytes=64) for a in range(PASSES)]
-        w4 = keep.tile([P, PASSES, 2 * N], U8, name="w4", align_bytes=64)
-        w4_sc = keep.tile([P, PASSES, N], U8, name="w4_sc", align_bytes=64)
-        factors = [keep.tile([P, T], F32, name="factors%d" % n, align_bytes=64) for n in range(GENE_TILES)]
-        v_q = keep.tile([P, S], U32, name="v_q", align_bytes=64)
-        v_sc = keep.tile([P, S], U8, name="v_sc", align_bytes=64)
-        h_bf = keep.tile([P, PASSES, S * PACK], BF16, name="h_bf", align_bytes=64)
-        h_q = keep.tile([P, PASSES, S], U32, name="h_q", align_bytes=64)
-        h_sc = keep.tile([P, PASSES, S], U8, name="h_sc", align_bytes=64)
-        rate = keep.tile([P, GENE_TILES, S], F32, name="rate", align_bytes=64)
-        count = keep.tile([P, GENE_TILES, S], F32, name="count", align_bytes=64)
-        res = keep.tile([P, GENE_TILES, S], F32, name="res", align_bytes=64)
+        table = keep.tile([P, T], U32, name="table", align_bytes=256)
+        table_sc = keep.tile([P, T], U8, name="table_sc", align_bytes=256)
+        w1_raw = [keep.tile([P, PACK, K_PASS], F32, name="w1_raw%d" % a, align_bytes=256) for a in range(PASSES)]
+        w1_bf = [keep.tile([P, PACK * K_PASS], BF16, name="w1_bf%d" % a, align_bytes=256) for a in range(PASSES)]
+        w1_q = [keep.tile([P, K_PASS], U32, name="w1_q%d" % a, align_bytes=256) for a in range(PASSES)]
+        w1_sc = [keep.tile([P, K_PASS], U8, name="w1_sc%d" % a, align_bytes=256) for a in range(PASSES)]
+        w4 = keep.tile([P, PASSES, 2 * N], U8, name="w4", align_bytes=256)
+        w4_sc = keep.tile([P, PASSES, N], U8, name="w4_sc", align_bytes=256)
+        factors = [keep.tile([P, T], F32, name="factors%d" % n, align_bytes=256) for n in range(GENE_TILES)]
+        v_q = keep.tile([P, S], U32, name="v_q", align_bytes=256)
+        v_sc = keep.tile([P, S], U8, name="v_sc", align_bytes=256)
+        h_bf = keep.tile([P, PASSES, S * PACK], BF16, name="h_bf", align_bytes=256)
+        h_q = keep.tile([P, PASSES, S], U32, name="h_q", align_bytes=256)
+        h_sc = keep.tile([P, PASSES, S], U8, name="h_sc", align_bytes=256)
+        rate = keep.tile([P, GENE_TILES, S], F32, name="rate", align_bytes=256)
+        count = keep.tile([P, GENE_TILES, S], F32, name="count", align_bytes=256)
+        res = keep.tile([P, GENE_TILES, S], F32, name="res", align_bytes=256)
         zero = keep.tile([P, 1], F32, name="zero")
         one_early = keep.tile([P, 1], F32, name="one_early")
         one_late = keep.tile([P, 2 * (GENE_TILES - 2) - 1], F32, name="one_late")
@@ -87,7 +87,7 @@ def tile_list_barcode_log_expression_kernel(tc, tab_words, tab_scales, offs, w1,
             elif engine == "vector":
                 nc.vector.tensor_copy(dst, src)
             else:
-                nc.gpsimd.tensor_scalar(dst.rearrange("p m j t -> p t m j"), src.rearrange("p m j t -> p t m j"),
+                nc.gpsimd.tensor_scalar(dst.rearrange("p m j t -> p m t j"), src.rearrange("p m j t -> p m t j"),
                                         1.0, 0.0, ALU.mult, ALU.add)
 
         def quantise_w1(a):
@@ -195,23 +195,24 @@ def tile_list_barcode_log_expression_kernel(tc, tab_words, tab_scales, offs, w1,
         for group in range(5):
             hidden_group(1, group, "scalar" if group % 2 else "vector", (group - 1) % 8)
         quantise_h(1, 0)
-        hidden_group(0, 7, "scalar", 4)
+        hidden_group(0, 7, "scalar", 7)
         hidden_group(1, 5, "scalar", 5)
-        hidden_group(1, 6, "vector", 7)
-        hidden_group(1, 7, "scalar", 6)
-        for n, bank in zip(range(3), (1, 0, 3)):
+        hidden(1, 6 * GROUP, SHARED, "vector", 4)
+        hidden(1, 6 * GROUP + SHARED, GROUP - SHARED, "scalar", 6)
+        hidden_group(1, 7, "scalar", 0)
+        for n, bank in zip(range(3), (1, 2, 3)):
             open_rates(n, 0, bank)
         quantise_h(0, 1)
         quantise_h(1, 1)
 
 
-        for n, bank in zip(range(4), (1, 0, 3, 2)):
+        for n, bank in zip(range(4), (1, 2, 3, 4)):
             rates(n, 0, bank)
-        for n, bank in zip(range(2), (4, 5)):
+        for n, bank in zip(range(2), (7, 5)):
             open_rates(n, 1, bank)
-        for n, bank in zip(range(4), (4, 5, 7, 6)):
+        for n, bank in zip(range(4), (7, 5, 6, 0)):
             rates(n, 1, bank)
-        for n, banks in zip(range(4, GENE_TILES), ((1, 0), (3, 2))):
+        for n, banks in zip(range(4, GENE_TILES), ((1, 2), (3, 4))):
             for half in range(2):
                 rates(n, half, banks[half])
         hold_logs()

@@ -32,7 +32,6 @@ W1_PIECES = (
 )
 WORD_PIECES = (256, 256, 512)
 LAST_PIECES = (512, 256, 192, 64)
-SHARED = GROUP // 2
 
 
 def pieces(widths):
@@ -197,22 +196,21 @@ def tile_list_barcode_log_expression_kernel(tc, tab_words, tab_scales, offs, w1,
         quantise_h(1, 0)
         hidden_group(0, 7, "scalar", 7)
         hidden_group(1, 5, "scalar", 5)
-        hidden(1, 6 * GROUP, SHARED, "vector", 4)
-        hidden(1, 6 * GROUP + SHARED, GROUP - SHARED, "scalar", 6)
-        hidden_group(1, 7, "scalar", 0)
-        for n, bank in zip(range(3), (1, 2, 3)):
+        hidden_group(1, 6, "vector", 4)
+        hidden_group(1, 7, "scalar", 6)
+        for n, bank in zip(range(3), (1, 0, 3)):
             open_rates(n, 0, bank)
         quantise_h(0, 1)
         quantise_h(1, 1)
 
 
-        for n, bank in zip(range(4), (1, 2, 3, 4)):
+        for n, bank in zip(range(4), (1, 0, 3, 2)):
             rates(n, 0, bank)
         for n, bank in zip(range(2), (7, 5)):
             open_rates(n, 1, bank)
-        for n, bank in zip(range(4), (7, 5, 6, 0)):
+        for n, bank in zip(range(4), (7, 5, 4, 6)):
             rates(n, 1, bank)
-        for n, banks in zip(range(4, GENE_TILES), ((1, 2), (3, 4))):
+        for n, banks in zip(range(4, GENE_TILES), ((1, 0), (3, 2))):
             for half in range(2):
                 rates(n, half, banks[half])
         hold_logs()

from contextlib import ExitStack

import concourse.mybir as mybir

K, H, N, T, S = 512, 1024, 768, 2048, 1024
FLOPS = 2 * K * H * S + 2 * H * N * S

F32 = mybir.dt.float32
BF16 = mybir.dt.bfloat16
I32 = mybir.dt.int32
U32 = mybir.dt.uint32
U16 = mybir.dt.uint16
U8 = mybir.dt.uint8
FP8X4 = mybir.dt.float8_e4m3fn_x4
FP4X4 = mybir.dt.float4_e2m1fn_x4
ACT = mybir.ActivationFunctionType
ALU = mybir.AluOpType

P = 128
PACK = 4
K_PASS = P * PACK
PASSES = H // K_PASS
GENE_TILES = N // P
HALF = S // 2
GROUP = P
SCALE_ROWS = 4
LIST_COLUMN = 16

W1_PIECES = (
    ((256, "scalar"), (256, "scalar")),
    ((128, "scalar"), (192, "gpsimd"), (192, "vector")),
)
WORD_PIECES = (256, 256, 512)
LAST_PIECES = (512, 256, 192, 64)


def pieces(widths):
    return [(sum(widths[:i]), width) for i, width in enumerate(widths)]


def span(start, width):
    return slice(start, start + width)


def tile_list_barcode_log_expression_kernel(tc, tab_words, tab_scales, offs, w1, w4_words, w4_scales, gT, out):
    nc = tc.nc
    with ExitStack() as ctx:
        keep = ctx.enter_context(tc.tile_pool(name="keep", bufs=1))
        psum = ctx.enter_context(tc.psum_pool(name="psum", bufs=1))

        offsets = keep.tile([P, S // LIST_COLUMN], U16, name="offsets")
        table = keep.tile([P, T], U32, name="table", align_bytes=256)
        table_sc = keep.tile([P, T], U8, name="table_sc", align_bytes=256)
        w1_raw = [keep.tile([P, PACK, K_PASS], F32, name="w1_raw%d" % a, align_bytes=256) for a in range(PASSES)]
        w1_bf = [keep.tile([P, PACK * K_PASS], BF16, name="w1_bf%d" % a, align_bytes=256) for a in range(PASSES)]
        w1_q = [keep.tile([P, K_PASS], U32, name="w1_q%d" % a, align_bytes=256) for a in range(PASSES)]
        w1_sc = [keep.tile([P, K_PASS], U8, name="w1_sc%d" % a, align_bytes=256) for a in range(PASSES)]
        w4 = keep.tile([P, PASSES, 2 * N], U8, name="w4", align_bytes=256)
        w4_sc = keep.tile([P, PASSES, N], U8, name="w4_sc", align_bytes=256)
        factors = [keep.tile([P, T], F32, name="factors%d" % n, align_bytes=256) for n in range(GENE_TILES)]
        v_q = keep.tile([P, S], U32, name="v_q", align_bytes=256)
        v_sc = keep.tile([P, S], U8, name="v_sc", align_bytes=256)
        h_bf = keep.tile([P, PASSES, S * PACK], BF16, name="h_bf", align_bytes=256)
        h_q = keep.tile([P, PASSES, S], U32, name="h_q", align_bytes=256)
        h_sc = keep.tile([P, PASSES, S], U8, name="h_sc", align_bytes=256)
        rate = keep.tile([P, GENE_TILES, S], F32, name="rate", align_bytes=256)
        count = keep.tile([P, GENE_TILES, S], F32, name="count", align_bytes=256)
        res = keep.tile([P, GENE_TILES, S], F32, name="res", align_bytes=256)
        zero = keep.tile([P, 1], F32, name="zero")
        one_early = keep.tile([P, 1], F32, name="one_early")
        one_late = keep.tile([P, 2 * (GENE_TILES - 2) - 1], F32, name="one_late")

        def listed(start, width):
            return offsets[:, start // LIST_COLUMN : (start + width) // LIST_COLUMN]

        def load_w1(a, start, width):
            rows = w1.rearrange("(p j) c -> p j c", j=PACK)
            nc.sync.dma_start(w1_raw[a][:, :, span(start, width)], rows[:, :, span(a * K_PASS + start, width)])

        def round_w1(a, start, width, engine):
            places = span(start // PACK, width // PACK)
            dst = w1_bf[a][:].rearrange("p (t m j) -> p m j t", t=PACK, j=PACK)[:, places]
            src = w1_raw[a][:].rearrange("p j (m t) -> p m j t", t=PACK)[:, places]
            if engine == "scalar":
                nc.scalar.copy(dst, src)
            elif engine == "vector":
                nc.vector.tensor_copy(dst, src)
            else:
                nc.gpsimd.tensor_scalar(dst.rearrange("p m j t -> p m t j"), src.rearrange("p m j t -> p m t j"),
                                        1.0, 0.0, ALU.mult, ALU.add)

        def quantise_w1(a):
            nc.vector.quantize_mx(w1_q[a][:].bitcast(FP8X4), w1_sc[a][:], w1_bf[a][:])

        def hidden(a, start, width, engine, bank):
            acc = psum.tile([P, PACK, width], F32, name="acc_h", tag="bank%d" % bank)
            cells = span(start, width)
            for t in range(PACK):
                places = span(t * P, P)
                nc.tensor.matmul_mx(acc[:, t, :], lhsT=w1_q[a][:, places].bitcast(FP8X4), lhsT_scale=w1_sc[a][:, places],
                                    rhs=v_q[:, cells].bitcast(FP8X4), rhs_scale=v_sc[:, cells], start=True, stop=True)
            dst = h_bf[:, a, span(start * PACK, width * PACK)].rearrange("p (c t) -> p c t", t=PACK)
            src = acc[:].rearrange("p t c -> p c t")
            if engine == "scalar":
                nc.scalar.activation(dst, src, ACT.Relu)
            else:
                nc.vector.tensor_scalar_max(dst, src, 0.0)

        def hidden_group(a, group, engine, bank):
            hidden(a, group * GROUP, GROUP, engine, bank)

        def quantise_h(a, half):
            cells = span(half * HALF, HALF)
            nc.vector.quantize_mx(h_q[:, a, cells].bitcast(FP8X4), h_sc[:, a, cells],
                                  h_bf[:, a, span(half * HALF * PACK, HALF * PACK)])

        def rate_of(n, start, width):
            if (n, start) == (1, 0):
                return count[:, 0, span(HALF, HALF)]
            return rate[:, n, span(start, width)]

        opened = {}

        def log_rate_pass(acc, n, half, a):
            cells = span(half * HALF, HALF)
            nc.tensor.matmul_mx(acc[:], lhsT=w4[:, a, span(n * 2 * P, 2 * P)].bitcast(FP4X4),
                                lhsT_scale=w4_sc[:, a, span(n * P, P)],
                                rhs=h_q[:, a, cells].bitcast(FP8X4), rhs_scale=h_sc[:, a, cells],
                                start=(a == 0), stop=(a == PASSES - 1))

        def open_rates(n, half, bank):
            acc = psum.tile([P, HALF], F32, name="acc_y", tag="bank%d" % bank)
            opened.setdefault((n, half), acc)
            log_rate_pass(acc, n, half, 0)

        def rates(n, half, bank):
            if (n, half) not in opened:
                open_rates(n, half, bank)
            acc = opened[n, half]
            log_rate_pass(acc, n, half, 1)
            nc.scalar.activation(rate_of(n, half * HALF, HALF), acc[:], ACT.Exp)

        def hold_logs():
            ends = rate[:].rearrange("p n c -> p (n c)")[:, 2 * S + HALF - 1 : GENE_TILES * S - HALF : HALF]
            nc.scalar.activation(one_late[:], ends, ACT.Sign, bias=one_early[:])

        def counts(n, start, width):
            nc.vector.tensor_tensor(count[:, n, span(start, width)], factors[n][:].indirect(listed(start, width)),
                                    rate_of(n, start, width), ALU.mult)

        def finish(n, start, width):
            cells = span(start, width)
            nc.scalar.activation(res[:, n, cells], count[:, n, cells], ACT.Ln, bias=one_late[:, 0:1])
            nc.sync.dma_start(out[span(n * P, P), cells], res[:, n, cells])

        nc.vector.memset(table_sc[:].bitcast(I32), 0)
        nc.vector.memset(zero[:], 0.0)
        nc.vector.memset(w4_sc[:].bitcast(I32), 0)
        nc.scalar.activation(one_early[:], zero[:], ACT.Exp)

        w1_pieces = [[(start, width, engine) for (start, width), (width, engine)
                      in zip(pieces([w for w, e in of_pass]), of_pass)] for of_pass in W1_PIECES]
        load_w1(0, *w1_pieces[0][0][:2])
        nc.sync.dma_start(offsets[:], offs)
        table_rows = tab_scales[0].rearrange("(q r) t -> r q t", r=SCALE_ROWS)
        for r in range(SCALE_ROWS):
            nc.sync.dma_start(table_sc[:].bitcast(I32)[r:P:32, :], table_rows[r].bitcast(I32))
        load_w1(0, *w1_pieces[0][1][:2])
        nc.sync.dma_start(table[:].bitcast(I32), tab_words[0].rearrange("p t i -> p (t i)").bitcast(I32))
        for start, width, engine in w1_pieces[1]:
            load_w1(1, start, width)
        w4_rows = w4_scales.rearrange("a (q r) c -> r q a c", r=SCALE_ROWS)
        for r in range(SCALE_ROWS):
            nc.sync.dma_start(w4_sc[:].bitcast(I32)[r:P:32, :, :], w4_rows[r].bitcast(I32))
        nc.sync.dma_start(w4[:].bitcast(I32), w4_words.rearrange("a p c -> p a c").bitcast(I32))
        for n in range(GENE_TILES):
            nc.sync.dma_start(factors[n][:], gT[span(n * P, P), :])

        for start, width, engine in w1_pieces[0]:
            round_w1(0, start, width, engine)
        nc.vector.tensor_copy(v_sc[:], table_sc[:].indirect(listed(0, S)))
        quantise_w1(0)
        for start, width in pieces(WORD_PIECES):
            nc.vector.tensor_copy(v_q[:, span(start, width)], table[:].indirect(listed(start, width)))
        for start, width, engine in w1_pieces[1]:
            round_w1(1, start, width, engine)
        quantise_w1(1)

        for group in range(4):
            hidden_group(0, group, "scalar", group)
        quantise_h(0, 0)
        for group in range(4, 7):
            hidden_group(0, group, "scalar", group)
        for group in range(5):
            hidden_group(1, group, "scalar" if group % 2 else "vector", (group - 1) % 8)
        quantise_h(1, 0)
        hidden_group(0, 7, "scalar", 7)
        hidden_group(1, 5, "scalar", 5)
        hidden_group(1, 6, "vector", 4)
        hidden_group(1, 7, "scalar", 6)
        for n, bank in zip(range(3), (1, 0, 3)):
            open_rates(n, 0, bank)
        quantise_h(0, 1)
        quantise_h(1, 1)


        for n, bank in zip(range(4), (1, 0, 3, 2)):
            rates(n, 0, bank)
        for n, bank in zip(range(2), (7, 5)):
            open_rates(n, 1, bank)
        for n, bank in zip(range(4), (7, 5, 4, 6)):
            rates(n, 1, bank)
        for n, banks in zip(range(4, GENE_TILES), ((1, 0), (3, 2))):
            for half in range(2):
                rates(n, half, banks[half])
        hold_logs()


        for half in range(2):
            for n in range(2):
                counts(n, half * HALF, HALF)
        for n in range(2, GENE_TILES - 1):
            counts(n, 0, S)
        for start, width in pieces(LAST_PIECES):
            counts(GENE_TILES - 1, start, width)

        for n in range(GENE_TILES - 2):
            finish(n, 0, S)
        for half in range(2):
            finish(GENE_TILES - 2, half * HALF, HALF)
        for start, width in pieces(LAST_PIECES):
            finish(GENE_TILES - 1, start, width)
